import numpy as np
import ml_dtypes


def mxq(x, axis, fmt="e4m3"):
    dtype, down = {"e4m3": (ml_dtypes.float8_e4m3fn, 7), "e5m2": (ml_dtypes.float8_e5m2, 14)}[fmt]
    v = np.moveaxis(np.asarray(x, np.float32).astype(ml_dtypes.bfloat16).astype(np.float64), axis, -1)
    blocks = v.reshape(v.shape[:-1] + (-1, 32))
    amax = np.abs(blocks).max(-1, keepdims=True)
    byte = np.maximum(np.where(amax > 0, np.frexp(amax)[1] - 1 + 127, 0) - down, 1)
    scale = np.exp2(byte - 127.0)
    codes = (blocks / scale).astype(np.float32).astype(dtype).astype(np.float64)
    return np.moveaxis((codes * scale).reshape(v.shape), -1, axis)


WIDE = False


def mx_kscale(k):
    if not WIDE:
        return np.ones(k)
    levels = np.array([10, -10, 5, -5, 0])
    if k % 512:
        return np.exp2(np.random.permutation(np.resize(levels, k // 32))).repeat(32)
    a = np.empty((k // 512, 16))
    for p in range(k // 512):
        a[p, :8] = np.random.permutation(np.resize(levels, 8))
        for g in range(8):
            far = levels[np.abs(levels - a[p, g]) >= 10]
            a[p, g + 8] = far[np.random.randint(len(far))]
    return np.exp2(a.ravel()).repeat(32)


BF16 = ml_dtypes.bfloat16


def bf(x):
    return np.asarray(x, np.float32).astype(BF16)


def f64(x):
    return np.asarray(x).astype(np.float64)


E2M1 = np.array([0.0, 0.5, 1.0, 1.5, 2.0, 3.0, 4.0, 6.0, -0.0, -0.5, -1.0, -1.5, -2.0, -3.0, -4.0, -6.0])


def pack_weight(w, fmt):
    k, n = w.shape
    w = f64(bf(w)).reshape(k // 32, 32, n)
    amax = np.abs(w).max(1)
    if fmt == "e4m3":
        byte = np.frexp(amax)[1] - 1 + 127 - 7
    else:
        mant, ex = np.frexp(amax / 6.0)
        byte = np.where(mant > 0.5, ex, ex - 1) + 127
    byte = np.clip(np.where(amax > 0, byte, 1), 1, 254)
    scaled = (w * np.exp2(127.0 - byte)[:, None, :]).reshape(k, n).astype(np.float32)
    by_word = np.ascontiguousarray(scaled.reshape(k // 512, 128, 4, n).transpose(0, 1, 3, 2))
    if fmt == "e4m3":
        words = by_word.astype(ml_dtypes.float8_e4m3fn).view(np.uint8)
    else:
        c = by_word.astype(ml_dtypes.float4_e2m1fn).view(np.uint8) & 0xF
        words = c[..., 0::2] | (c[..., 1::2] << 4)
    return np.ascontiguousarray(words), np.ascontiguousarray(byte.astype(np.uint8).reshape(k // 512, 16, n))


def unpack_weight(words, scales, fmt):
    g, p, n, _ = words.shape
    if fmt == "e4m3":
        vals = np.ascontiguousarray(words).view(ml_dtypes.float8_e4m3fn).astype(np.float64)
    else:
        nib = np.empty((g, p, n, 4), np.uint8)
        nib[..., 0::2] = words & 0xF
        nib[..., 1::2] = words >> 4
        vals = E2M1[nib]
    vals = vals * np.repeat(np.exp2(scales.astype(np.float64) - 127.0), 8, axis=1)[..., None]
    return vals.transpose(0, 1, 3, 2).reshape(g * 512, n)
def pack4(w):
    words, scales = pack_weight(w, "e2m1")
    return words.reshape(words.shape[0], 128, -1), scales


def unpack4(words, scales):
    return unpack_weight(words.reshape(words.shape[0], 128, -1, 2), scales, "e2m1")


E4M3FN = np.array([(-1.0 if i & 128 else 1.0) * ((1.0 + (i & 7) / 8.0) * 2.0 ** (((i >> 3) & 15) - 7) if i & 120 else (i & 7) * 2.0 ** -9) for i in range(256)])


def e4m3fn_bytes(y):
    return np.clip(np.asarray(y, np.float64), -448.0, 448.0).astype(np.float32).astype(ml_dtypes.float8_e4m3fn).view(np.uint8)


def e4m3fn_values(b):
    return E4M3FN[b]


X, N, Q = 2048, 512, 1024


def entropy_ansatz(alpha, m):
    eta = mxq(alpha, 1, "e4m3") @ m
    return np.exp(eta)


def upwind_face_flux(f, w):
    fp = np.roll(f, -1, axis=0)
    w_pos = np.maximum(w, 0.0)[None, :]
    w_neg = np.minimum(w, 0.0)[None, :]
    return w_pos * f + w_neg * fp


def draw0():
    s, t = mx_kscale(N), mx_kscale(Q)
    alpha = bf(np.random.standard_normal((X, N)) * 0.5 / np.sqrt(N) * s[None, :])
    m_words, m_scales = pack4(np.random.standard_normal((N, Q)) / s[:, None])
    w = bf(np.random.standard_normal(Q) * t)
    p_words, p_scales = pack4(np.random.standard_normal((Q, N)) * 2.0 / np.sqrt(Q) / t[:, None])
    return {
        "alpha": alpha,
        "m_words": m_words,
        "m_scales": m_scales,
        "w": w,
        "p_words": p_words,
        "p_scales": p_scales,
        "u": bf(np.random.standard_normal((X, N))),
        "sigma": bf(np.random.uniform(0.1, 1.0, X)),
    }


def core(alpha, m_words, m_scales, w, p_words, p_scales, u, sigma):
    f = entropy_ansatz(f64(alpha), unpack4(m_words, m_scales))
    flux = upwind_face_flux(f, f64(w))
    d = flux - np.roll(flux, 1, axis=0)
    div = mxq(d, 1, "e4m3") @ unpack4(p_words, p_scales)
    return (f64(u) - 0.5 * div) / (1.0 + f64(sigma))[:, None]


def setup_inputs():
    drawn = draw0()
    full = np.asarray(drawn['alpha']).astype(np.float64)
    scale = (np.abs(full).reshape(16, 128, 4, 128).max(axis=(1, 3)) / 448.0).astype(np.float32)
    given = {}
    for key, value in drawn.items():
        if key == 'alpha':
            given['alpha_bytes'] = e4m3fn_bytes(full / np.repeat(np.repeat(scale.astype(np.float64), 128, axis=0), 128, axis=1))
            given['alpha_scale'] = scale
        else:
            given[key] = value
    return given


def reference(alpha_bytes, alpha_scale, m_words, m_scales, w, p_words, p_scales, u, sigma):
    return core(e4m3fn_values(alpha_bytes) * np.repeat(np.repeat(alpha_scale.astype(np.float64), 128, axis=0), 128, axis=1), m_words, m_scales, w, p_words, p_scales, u, sigma)

@@ -1,0 +1,290 @@
+from contextlib import ExitStack
+
+import concourse.mybir as mybir
+from concourse.masks import make_identity
+
+P = 128
+X, N, Q = 2048, 512, 1024
+FLOPS = 2 * X * N * Q * 2
+
+F32 = mybir.dt.float32
+BF16 = mybir.dt.bfloat16
+I32 = mybir.dt.int32
+U32 = mybir.dt.uint32
+U8 = mybir.dt.uint8
+FP8 = mybir.dt.float8_e4m3fn
+FP8X4 = mybir.dt.float8_e4m3fn_x4
+FP4X4 = mybir.dt.float4_e2m1fn_x4
+ALU = mybir.AluOpType
+ACT = mybir.ActivationFunctionType
+AX = mybir.AxisListType
+
+R = 16
+RC = 4
+NCH = R // RC
+G = 2
+T4 = 4
+J = G * T4
+FS = 132
+
+WIDEN_SCALAR = (3,)
+INTERLEAVE_VECTOR = ()
+
+
+def tile_entropyclosuremomentkineticupwindstep_d2p_kernel(
+    tc, alpha_bytes, alpha_scale, m_words, m_scales, w, p_words, p_scales, u, sigma, out
+):
+    nc = tc.nc
+    alpha_v = alpha_bytes.rearrange("(p r) k -> p r k", r=R)
+    u_v = u.rearrange("(p r) n -> p r n", r=R)
+    out_v = out.rearrange("(p r) n -> p r n", r=R)
+    sigma_v = sigma.rearrange("(p r) -> p r", r=R)
+
+    with ExitStack() as ctx:
+        keep = ctx.enter_context(tc.tile_pool(name="keep", bufs=1))
+        front_pool = ctx.enter_context(tc.tile_pool(name="front", bufs=2))
+        t_pool = ctx.enter_context(tc.tile_pool(name="tpool", bufs=5))
+        d_pool = ctx.enter_context(tc.tile_pool(name="dpool", bufs=2))
+        q_pool = ctx.enter_context(tc.tile_pool(name="qpool", bufs=4))
+        o_pool = ctx.enter_context(tc.tile_pool(name="opool", bufs=4))
+        ps_t = ctx.enter_context(tc.psum_pool(name="ps_t", bufs=2))
+        ps_e = ctx.enter_context(tc.psum_pool(name="ps_e", bufs=4))
+        ps_o = ctx.enter_context(tc.psum_pool(name="ps_o", bufs=2))
+
+        ident = keep.tile([P, P], F32)
+        make_identity(nc, ident[:])
+
+        sc_all = keep.tile([P, 64], F32)
+        nc.sync.dma_start(out=sc_all[:], in_=alpha_scale.rearrange("i j -> (i j)").partition_broadcast(P))
+        a_raw = keep.tile([P, R, N], U8, align_bytes=64)
+        nc.sync.dma_start(out=a_raw[:, 0:RC, :], in_=alpha_v[:, 0:RC, :])
+
+        w_sb = keep.tile([P, J], BF16)
+        nc.scalar.dma_start(out=w_sb[:].rearrange("p (g t) -> p g t", t=T4), in_=w.rearrange("(g p t) -> p g t", p=P, t=T4))
+        m_raw = keep.tile([P, 2 * Q], U8, align_bytes=64)
+        nc.scalar.dma_start(out=m_raw[:].bitcast(I32), in_=m_words[0].bitcast(I32))
+        ms_raw = keep.tile([P, Q], U8, align_bytes=64)
+        nc.vector.memset(ms_raw[:].bitcast(I32), 0)
+        for qd in range(4):
+            nc.scalar.dma_start(
+                out=ms_raw[32 * qd : 32 * qd + 4, :].bitcast(I32), in_=m_scales[0, 4 * qd : 4 * qd + 4, :].bitcast(I32)
+            )
+        sg = keep.tile([P, 2 * R], BF16)
+        nc.scalar.dma_start(out=sg[:, 0:R], in_=sigma_v)
+        nc.scalar.dma_start(out=sg[0 : P - 1, R : 2 * R], in_=sigma_v[1:P, :])
+        nc.scalar.dma_start(out=sg[P - 1 : P, R : 2 * R], in_=sigma_v[0:1, :])
+
+        for c in range(1, NCH):
+            nc.sync.dma_start(out=a_raw[:, RC * c : RC * (c + 1), :], in_=alpha_v[:, RC * c : RC * (c + 1), :])
+        p_raw = keep.tile([P, G, 2 * N], U8, align_bytes=64)
+        for g in range(G):
+            nc.sync.dma_start(out=p_raw[:, g, :].bitcast(I32), in_=p_words[g].bitcast(I32))
+        ps_raw = keep.tile([P, G, N], U8, align_bytes=64)
+        nc.vector.memset(ps_raw[:].rearrange("p g n -> p (g n)").bitcast(I32), 0)
+        for g in range(G):
+            for qd in range(4):
+                nc.sync.dma_start(
+                    out=ps_raw[32 * qd : 32 * qd + 4, g, :].bitcast(I32), in_=p_scales[g, 4 * qd : 4 * qd + 4, :].bitcast(I32)
+                )
+        u_sb = keep.tile([P, R, N], BF16)
+        for lo, hi in ((1, 4), (4, 8), (8, 12), (12, 16)):
+            nc.sync.dma_start(out=u_sb[:, lo - 1 : hi - 1, :], in_=u_v[:, lo:hi, :])
+        nc.sync.dma_start(out=u_sb[0 : P - 1, R - 1, :], in_=u_v[1:P, 0, :])
+        nc.sync.dma_start(out=u_sb[P - 1 : P, R - 1, :], in_=u_v[0:1, 0, :])
+
+        m16 = keep.tile([P, R], F32)
+        nc.vector.tensor_reduce(out=m16[:], in_=ident[:].rearrange("p (i b) -> p i b", b=8), axis=AX.X, op=ALU.add)
+        sc_sel = keep.tile([P, 4, R], F32)
+        for j in range(4):
+            nc.vector.tensor_tensor(
+                out=sc_sel[:, j, :], in0=sc_all[:].rearrange("p (i j) -> p j i", j=4)[:, j, :], in1=m16[:], op=ALU.mult
+            )
+        sc = keep.tile([P, 4], F32)
+        nc.vector.tensor_reduce(out=sc[:], in_=sc_sel[:], axis=AX.X, op=ALU.add)
+
+        w_abs = keep.tile([P, J], F32)
+        nc.scalar.activation(out=w_abs[:], in_=w_sb[:], func=ACT.Abs)
+        w_cl = keep.tile([P, J], F32)
+        nc.vector.tensor_scalar(out=w_cl[:], in0=w_abs[:], scalar1=2.0**-60, scalar2=2.0**60, op0=ALU.max, op1=ALU.min)
+        w_ln = keep.tile([P, J], F32)
+        nc.scalar.activation(out=w_ln[:], in_=w_cl[:], func=ACT.Ln)
+        n_pos = keep.tile([P, J], F32)
+        nc.vector.tensor_scalar(out=n_pos[:], in0=w_sb[:], scalar1=0.0, scalar2=-1.0, op0=ALU.is_gt, op1=ALU.mult)
+        n_neg = keep.tile([P, J], F32)
+        nc.vector.tensor_scalar(out=n_neg[:], in0=w_sb[:], scalar1=0.0, scalar2=-1.0, op0=ALU.is_lt, op1=ALU.mult)
+
+        one_sg = keep.tile([P, 2 * R], F32)
+        nc.vector.tensor_scalar(out=one_sg[:], in0=sg[:], scalar1=1.0, scalar2=None, op0=ALU.add)
+        rr = keep.tile([P, 2 * R], F32)
+        nc.vector.reciprocal(out=rr[:], in_=one_sg[:])
+        cc = keep.tile([P, 2 * R], F32)
+        nc.vector.tensor_scalar(out=cc[:], in0=rr[:], scalar1=-0.5, scalar2=None, op0=ALU.mult)
+
+        m_w = keep.tile([P, J, 2 * P], U8, align_bytes=64)
+        m_s = keep.tile([P, J, P], U8, align_bytes=64)
+        for g in range(G):
+            for t in range(T4):
+                j = T4 * g + t
+                nc.vector.tensor_copy(
+                    out=m_w[:, j, :].rearrange("p (m b) -> p m b", b=2),
+                    in_=m_raw[:, 1024 * g : 1024 * (g + 1)].rearrange("p (m t b) -> p t m b", t=T4, b=2)[:, t, :, :],
+                )
+                nc.gpsimd.tensor_copy(
+                    out=m_s[:, j, :],
+                    in_=ms_raw[:, 512 * g : 512 * (g + 1)].rearrange("p (m t) -> p t m", t=T4)[:, t, :],
+                )
+
+        f_sb = keep.tile([P, J, R, FS], F32)
+        ur = keep.tile([P, R, N], F32)
+
+        def front(c):
+            xb = front_pool.tile([P, RC, N], BF16, name="xb")
+            for r in range(RC):
+                for j in range(4):
+                    src = a_raw[:, RC * c + r, P * j : P * (j + 1)].bitcast(FP8)
+                    dst = xb[:, r, P * j : P * (j + 1)]
+                    if r in WIDEN_SCALAR:
+                        nc.scalar.activation(out=dst, in_=src, func=ACT.Copy, scale=sc[:, j : j + 1])
+                    else:
+                        nc.vector.tensor_scalar(out=dst, in0=src, scalar1=sc[:, j : j + 1], scalar2=None, op0=ALU.mult)
+            ag = front_pool.tile([P, RC * P * T4], BF16, name="ag", align_bytes=64)
+            for h in range(2):
+                bank = ps_t.tile([P, 2, 2, P], F32, name="bank")
+                for rr2 in range(2):
+                    words = xb[:, 2 * h + rr2, :].bitcast(F32)
+                    for v in range(2):
+                        nc.tensor.transpose(bank[:, rr2, v, :], words[:, v : 2 * P : 2], ident[:])
+                nc.scalar.copy(
+                    out=ag[:, 1024 * h : 1024 * (h + 1)].bitcast(F32).rearrange("p (r x v) -> p r x v", r=2, v=2),
+                    in_=bank[:].rearrange("p r v x -> p r x v"),
+                )
+            ac = front_pool.tile([P, RC * P], U32, name="ac", align_bytes=64)
+            asc = front_pool.tile([P, RC * P], U8, name="asc", align_bytes=64)
+            nc.vector.quantize_mx(out=ac[:].bitcast(FP8X4), scales=asc[:], in_=ag[:])
+            return ac, asc
+
+        def first(c, ac, asc):
+            for j in range(J):
+                eta = ps_e.tile([P, RC * P], F32, name="eta")
+                nc.tensor.matmul_mx(
+                    out=eta[:],
+                    lhsT=m_w[:, j, :].bitcast(FP4X4),
+                    lhsT_scale=m_s[:, j, :],
+                    rhs=ac[:].bitcast(FP8X4),
+                    rhs_scale=asc[:],
+                    start=True,
+                    stop=True,
+                )
+                nc.scalar.activation(
+                    out=f_sb[:, j, RC * c : RC * (c + 1), 0:P],
+                    in_=eta[:].rearrange("p (r x) -> p r x", r=RC),
+                    func=ACT.Exp,
+                    bias=w_ln[:, j : j + 1],
+                )
+
+        def diff(a, b, g):
+            nb = b - a + 1
+            d = d_pool.tile([P, T4, 6 * P], BF16, name="d")
+            tts = []
+            for t in range(T4):
+                j = T4 * g + t
+                tt = t_pool.tile([P, 6 * P], F32, name="tt")
+                tts.append(tt)
+                nreg = min(b, R - 2) - a + 1
+                nc.vector.scalar_tensor_tensor(
+                    out=tt[:, 0 : nreg * P].rearrange("p (r x) -> p r x", x=P),
+                    in0=f_sb[:, j, a + 1 : a + nreg + 1, 0:P],
+                    scalar=n_neg[:, j : j + 1],
+                    in1=f_sb[:, j, a : a + nreg, 0:P],
+                    op0=ALU.mult,
+                    op1=ALU.add,
+                )
+                if b == R:
+                    nc.vector.scalar_tensor_tensor(
+                        out=tt[:, nreg * P : (nreg + 1) * P],
+                        in0=f_sb[:, j, 0, 1 : P + 1],
+                        scalar=n_neg[:, j : j + 1],
+                        in1=f_sb[:, j, R - 1, 0:P],
+                        op0=ALU.mult,
+                        op1=ALU.add,
+                    )
+                    nc.vector.scalar_tensor_tensor(
+                        out=tt[:, (nreg + 1) * P : (nreg + 2) * P],
+                        in0=f_sb[:, j, 1, 1 : P + 1],
+                        scalar=n_neg[:, j : j + 1],
+                        in1=f_sb[:, j, 0, 1 : P + 1],
+                        op0=ALU.mult,
+                        op1=ALU.add,
+                    )
+            for t in range(T4):
+                j = T4 * g + t
+                nc.vector.scalar_tensor_tensor(
+                    out=d[:, t, 0 : nb * P].rearrange("p (r x) -> p r x", x=P),
+                    in0=f_sb[:, j, a - 1 : b, 0:P],
+                    scalar=n_pos[:, j : j + 1],
+                    in1=tts[t][:, 0 : nb * P].rearrange("p (r x) -> p r x", x=P),
+                    op0=ALU.mult,
+                    op1=ALU.add,
+                )
+            dil = d_pool.tile([P, 6 * P, T4], BF16, name="dil", align_bytes=64)
+            dc = q_pool.tile([P, 6 * P], U32, name="dc", align_bytes=64)
+            ds = q_pool.tile([P, 6 * P], U8, name="ds", align_bytes=64)
+            for k in range(nb // 2):
+                cols = slice(2 * P * k, 2 * P * (k + 1))
+                dst = dil[:, cols, :].rearrange("p (c i) t -> p c t i", i=4)
+                src = d[:, :, cols].rearrange("p t (c i) -> p c t i", i=4)
+                if (a, g, k) in INTERLEAVE_VECTOR:
+                    nc.vector.tensor_copy(out=dst, in_=src)
+                else:
+                    nc.scalar.copy(out=dst, in_=src)
+                nc.vector.quantize_mx(
+                    out=dc[:, cols].bitcast(FP8X4), scales=ds[:, cols], in_=dil[:, cols, :].rearrange("p x t -> p (x t)")
+                )
+            return dc, ds
+
+        def second(a, b, ops):
+            for k in range((b - a + 1) // 2):
+                o = o_pool.tile([P, 2, N], F32, name="o")
+                for i in range(2):
+                    blk = a + 2 * k + i
+                    cols = slice(P * (2 * k + i), P * (2 * k + i + 1))
+                    acc = ps_o.tile([P, N], F32, name="acc")
+                    for g in range(G):
+                        nc.tensor.matmul_mx(
+                            out=acc[:],
+                            lhsT=ops[g][0][:, cols].bitcast(FP8X4),
+                            lhsT_scale=ops[g][1][:, cols],
+                            rhs=p_raw[:, g, :].bitcast(FP4X4),
+                            rhs_scale=ps_raw[:, g, :],
+                            start=(g == 0),
+                            stop=(g == G - 1),
+                        )
+                    nc.vector.scalar_tensor_tensor(
+                        out=o[:, i, :], in0=acc[:], scalar=cc[:, blk : blk + 1], in1=ur[:, blk - 1, :], op0=ALU.mult, op1=ALU.add
+                    )
+                lo = a + 2 * k
+                if lo + 1 < R:
+                    nc.sync.dma_start(out=out_v[:, lo : lo + 2, :], in_=o[:])
+                else:
+                    nc.sync.dma_start(out=out_v[:, lo, :], in_=o[:, 0, :])
+                    nc.sync.dma_start(out=out_v[1:P, 0, :], in_=o[0 : P - 1, 1, :])
+                    nc.sync.dma_start(out=out_v[0:1, 0, :], in_=o[P - 1 : P, 1, :])
+
+        def scale_u(lo, hi):
+            for i in range(lo, hi):
+                nc.scalar.activation(out=ur[:, i, :], in_=u_sb[:, i, :], func=ACT.Copy, scale=rr[:, i + 1 : i + 2])
+
+        windows = ((1, 2), (3, 6), (7, 10), (11, 16))
+        ac, asc = front(0)
+        first(0, ac, asc)
+        for j in range(J):
+            nc.vector.tensor_copy(out=f_sb[:, j, 0:2, P : P + 1], in_=f_sb[:, j, 0:2, 0:1])
+        for c in range(NCH):
+            if c + 1 < NCH:
+                ac, asc = front(c + 1)
+            a, b = windows[c]
+            scale_u(a - 1, b)
+            ops = [diff(a, b, g) for g in range(G)]
+            if c + 1 < NCH:
+                first(c + 1, ac, asc)
+            second(a, b, ops)

@@ -20,15 +20,13 @@ ACT = mybir.ActivationFunctionType
 AX = mybir.AxisListType
 
 R = 16
-RC = 4
-NCH = R // RC
+CHUNKS = ((0, 2), (2, 4), (4, 8), (8, 12), (12, 16))
 G = 2
 T4 = 4
 J = G * T4
-FS = 132
 
-WIDEN_SCALAR = (3,)
-INTERLEAVE_VECTOR = ()
+WIDEN_SCALAR = ()
+IL_WINDOWS = ((1, 2), (3, 4))
 
 
 def tile_entropyclosuremomentkineticupwindstep_d2p_kernel(
@@ -43,53 +41,57 @@ def tile_entropyclosuremomentkineticupwindstep_d2p_kernel(
     with ExitStack() as ctx:
         keep = ctx.enter_context(tc.tile_pool(name="keep", bufs=1))
         front_pool = ctx.enter_context(tc.tile_pool(name="front", bufs=2))
-        t_pool = ctx.enter_context(tc.tile_pool(name="tpool", bufs=5))
         d_pool = ctx.enter_context(tc.tile_pool(name="dpool", bufs=2))
-        q_pool = ctx.enter_context(tc.tile_pool(name="qpool", bufs=4))
+        q_pool = ctx.enter_context(tc.tile_pool(name="qpool", bufs=3))
         o_pool = ctx.enter_context(tc.tile_pool(name="opool", bufs=4))
         ps_t = ctx.enter_context(tc.psum_pool(name="ps_t", bufs=2))
         ps_e = ctx.enter_context(tc.psum_pool(name="ps_e", bufs=4))
         ps_o = ctx.enter_context(tc.psum_pool(name="ps_o", bufs=2))
 
-        ident = keep.tile([P, P], F32)
-        make_identity(nc, ident[:])
+        warm = keep.tile([P, 1], F32)
+        nc.vector.memset(warm[:], 1.0)
+        w_ln = keep.tile([P, 3 * J], F32)
+        nc.scalar.activation(out=w_ln[:, 0:1], in_=warm[:], func=ACT.Ln)
 
+        a_raw = keep.tile([P, R, N], U8, align_bytes=64)
+        w_sb = keep.tile([P, J], BF16)
+        nc.sync.dma_start(out=w_sb[:].rearrange("p (g t) -> p g t", t=T4), in_=w.rearrange("(g p t) -> p g t", p=P, t=T4))
         sc_all = keep.tile([P, 64], F32)
         nc.sync.dma_start(out=sc_all[:], in_=alpha_scale.rearrange("i j -> (i j)").partition_broadcast(P))
-        a_raw = keep.tile([P, R, N], U8, align_bytes=64)
-        nc.sync.dma_start(out=a_raw[:, 0:RC, :], in_=alpha_v[:, 0:RC, :])
-
-        w_sb = keep.tile([P, J], BF16)
-        nc.scalar.dma_start(out=w_sb[:].rearrange("p (g t) -> p g t", t=T4), in_=w.rearrange("(g p t) -> p g t", p=P, t=T4))
-        m_raw = keep.tile([P, 2 * Q], U8, align_bytes=64)
-        nc.scalar.dma_start(out=m_raw[:].bitcast(I32), in_=m_words[0].bitcast(I32))
+        for lo, hi in CHUNKS[0:1]:
+            nc.sync.dma_start(out=a_raw[:, lo:hi, :], in_=alpha_v[:, lo:hi, :])
         ms_raw = keep.tile([P, Q], U8, align_bytes=64)
         nc.vector.memset(ms_raw[:].bitcast(I32), 0)
+        ps_raw = keep.tile([P, G, N], U8, align_bytes=64)
+        nc.vector.memset(ps_raw[:].rearrange("p g n -> p (g n)").bitcast(I32), 0)
+        m_raw = keep.tile([P, 2 * Q], U8, align_bytes=64)
+        nc.sync.dma_start(out=m_raw[:].bitcast(I32), in_=m_words[0].bitcast(I32))
         for qd in range(4):
-            nc.scalar.dma_start(
+            nc.sync.dma_start(
                 out=ms_raw[32 * qd : 32 * qd + 4, :].bitcast(I32), in_=m_scales[0, 4 * qd : 4 * qd + 4, :].bitcast(I32)
             )
+        ident = keep.tile([P, P], F32)
+        make_identity(nc, ident[:])
+        for lo, hi in CHUNKS[1:]:
+            nc.sync.dma_start(out=a_raw[:, lo:hi, :], in_=alpha_v[:, lo:hi, :])
         sg = keep.tile([P, 2 * R], BF16)
-        nc.scalar.dma_start(out=sg[:, 0:R], in_=sigma_v)
-        nc.scalar.dma_start(out=sg[0 : P - 1, R : 2 * R], in_=sigma_v[1:P, :])
-        nc.scalar.dma_start(out=sg[P - 1 : P, R : 2 * R], in_=sigma_v[0:1, :])
-
-        for c in range(1, NCH):
-            nc.sync.dma_start(out=a_raw[:, RC * c : RC * (c + 1), :], in_=alpha_v[:, RC * c : RC * (c + 1), :])
+        nc.sync.dma_start(out=sg[:, 0:R], in_=sigma_v)
+        for lo, hi in ((1, 113), (113, P)):
+            nc.sync.dma_start(out=sg[lo - 1 : hi - 1, R : 2 * R], in_=sigma_v[lo:hi, :])
+        nc.sync.dma_start(out=sg[P - 1 : P, R : 2 * R], in_=sigma_v[0:1, :])
         p_raw = keep.tile([P, G, 2 * N], U8, align_bytes=64)
         for g in range(G):
             nc.sync.dma_start(out=p_raw[:, g, :].bitcast(I32), in_=p_words[g].bitcast(I32))
-        ps_raw = keep.tile([P, G, N], U8, align_bytes=64)
-        nc.vector.memset(ps_raw[:].rearrange("p g n -> p (g n)").bitcast(I32), 0)
         for g in range(G):
             for qd in range(4):
                 nc.sync.dma_start(
                     out=ps_raw[32 * qd : 32 * qd + 4, g, :].bitcast(I32), in_=p_scales[g, 4 * qd : 4 * qd + 4, :].bitcast(I32)
                 )
         u_sb = keep.tile([P, R, N], BF16)
-        for lo, hi in ((1, 4), (4, 8), (8, 12), (12, 16)):
+        for lo, hi in ((1, 5), (5, 9), (9, 13), (13, R)):
             nc.sync.dma_start(out=u_sb[:, lo - 1 : hi - 1, :], in_=u_v[:, lo:hi, :])
-        nc.sync.dma_start(out=u_sb[0 : P - 1, R - 1, :], in_=u_v[1:P, 0, :])
+        for lo, hi in ((1, 113), (113, P)):
+            nc.sync.dma_start(out=u_sb[lo - 1 : hi - 1, R - 1, :], in_=u_v[lo:hi, 0, :])
         nc.sync.dma_start(out=u_sb[P - 1 : P, R - 1, :], in_=u_v[0:1, 0, :])
 
         m16 = keep.tile([P, R], F32)
@@ -102,17 +104,293 @@ def tile_entropyclosuremomentkineticupwindstep_d2p_kernel(
         sc = keep.tile([P, 4], F32)
         nc.vector.tensor_reduce(out=sc[:], in_=sc_sel[:], axis=AX.X, op=ALU.add)
 
+        a_sb = keep.tile([P, T4, (R + 1) * P], F32)
+        b_sb = keep.tile([P, T4, R * P], F32)
+        f_sb = keep.tile([P, T4, R * P], F32)
+        dd = keep.tile([P, T4, (R + 1) * P], BF16)
+
+        ac = keep.tile([P, X], U32, align_bytes=64)
+        asc = keep.tile([P, X], U8, align_bytes=64)
+
+        def widen(c):
+            lo, hi = CHUNKS[c]
+            xb = front_pool.tile([P, 4, N], BF16, name="xb", bufs=4)
+            for r in range(lo, hi):
+                for j in range(4):
+                    src = a_raw[:, r, P * j : P * (j + 1)].bitcast(FP8)
+                    dst = xb[:, r - lo, P * j : P * (j + 1)]
+                    if r in WIDEN_SCALAR:
+                        nc.scalar.activation(out=dst, in_=src, func=ACT.Copy, scale=sc[:, j : j + 1])
+                    else:
+                        nc.vector.tensor_scalar(out=dst, in0=src, scalar1=sc[:, j : j + 1], scalar2=None, op0=ALU.mult)
+            return xb
+
+        def turn(c, xb):
+            lo, hi = CHUNKS[c]
+            ag = front_pool.tile([P, 4 * P * T4], BF16, name="ag", align_bytes=64)
+            for h in range((hi - lo) // 2):
+                bank = ps_t.tile([P, 4, P], F32, name="bank")
+                for i in range(2):
+                    words = xb[:, 2 * h + i, :].bitcast(F32)
+                    for v in range(2):
+                        nc.tensor.transpose(bank[:, 2 * i + v, :], words[:, v : 2 * P : 2], ident[:])
+                nc.scalar.copy(
+                    out=ag[:, 1024 * h : 1024 * (h + 1)].bitcast(F32).rearrange("p (r x v) -> p r x v", r=2, v=2),
+                    in_=bank[:].rearrange("p (r v) x -> p r x v", r=2),
+                )
+            return ag
+
+        def quant_a(c, ag):
+            lo, hi = CHUNKS[c]
+            nn = (hi - lo) * P
+            nc.vector.quantize_mx(
+                out=ac[:, P * lo : P * hi].bitcast(FP8X4), scales=asc[:, P * lo : P * hi], in_=ag[:, 0 : T4 * nn]
+            )
+
+
+        m_w = keep.tile([P, J, 2 * P], U8, align_bytes=64)
+        m_s = keep.tile([P, J, P], U8, align_bytes=64)
+
+        def permute(g):
+            nc.vector.tensor_copy(
+                out=m_s[:, T4 * g : T4 * (g + 1), :],
+                in_=ms_raw[:, 512 * g : 512 * (g + 1)].rearrange("p (m t) -> p t m", t=T4),
+            )
+            for t in range(T4):
+                j = T4 * g + t
+                nc.vector.tensor_copy(
+                    out=m_w[:, j, :].rearrange("p (m b) -> p m b", b=2),
+                    in_=m_raw[:, 1024 * g : 1024 * (g + 1)].rearrange("p (m t b) -> p t m b", t=T4, b=2)[:, t, :, :],
+                )
+
+        def first(c, g):
+            lo, hi = CHUNKS[c]
+            nn = (hi - lo) * P
+            cols = slice(P * lo, P * hi)
+            for t in range(T4):
+                j = T4 * g + t
+                bank_e = ps_e.tile([P, 4 * P], F32, name="bank_e")
+                eta = bank_e[:, 0:nn]
+                nc.tensor.matmul_mx(
+                    out=eta,
+                    lhsT=m_w[:, j, :].bitcast(FP4X4),
+                    lhsT_scale=m_s[:, j, :],
+                    rhs=ac[:, cols].bitcast(FP8X4),
+                    rhs_scale=asc[:, cols],
+                    start=True,
+                    stop=True,
+                )
+                if g == 0:
+                    nc.scalar.activation(out=a_sb[:, t, cols], in_=eta, func=ACT.Exp, bias=w_ln[:, J + t : J + t + 1])
+                    nc.scalar.activation(out=b_sb[:, t, cols], in_=eta, func=ACT.Exp, bias=w_ln[:, 2 * J + t : 2 * J + t + 1])
+                else:
+                    nc.scalar.activation(out=f_sb[:, t, cols], in_=eta, func=ACT.Exp, bias=w_ln[:, j : j + 1])
+
+        def halo(tile_ap, src, dst):
+            nc.vector.tensor_copy(out=tile_ap[:, :, P * dst : P * dst + P - 1], in_=tile_ap[:, :, P * src + 1 : P * (src + 1)])
+            nc.vector.tensor_copy(out=tile_ap[:, :, P * dst + P - 1 : P * (dst + 1)], in_=tile_ap[:, :, P * src : P * src + 1])
+
+        def shifted(out, in0, in1):
+            for dst, src in ((slice(0, P - 1), slice(1, P)), (slice(P - 1, P), slice(0, 1))):
+                pick = []
+                for operand in (in0, in1):
+                    ap, blk, moved = operand
+                    cols = src if moved else dst
+                    pick.append(ap[:, :, P * blk + cols.start : P * blk + cols.stop])
+                nc.vector.tensor_tensor(out=out[0][:, :, P * out[1] + dst.start : P * out[1] + dst.stop], in0=pick[0], in1=pick[1], op=ALU.subtract)
+
+        def flux(lo, hi):
+            top = min(hi, R - 2)
+            nc.vector.tensor_tensor(
+                out=a_sb[:, :, P * lo : P * (top + 1)],
+                in0=a_sb[:, :, P * lo : P * (top + 1)],
+                in1=b_sb[:, :, P * (lo + 1) : P * (top + 2)],
+                op=ALU.subtract,
+            )
+            if hi == R - 1:
+                shifted((a_sb, R - 1), (a_sb, R - 1, False), (b_sb, 0, True))
+
+        def four(ap):
+            return ap.rearrange("p t (c i) -> p c t i", i=4)
+
+        def four_out(ap):
+            return ap.rearrange("p (c i) t -> p c t i", i=4)
+
+        def steps(lo, hi):
+            top = min(hi, R - 2)
+            nc.vector.tensor_tensor(
+                out=dd[:, :, P * lo : P * (top + 1)],
+                in0=f_sb[:, :, P * (lo + 1) : P * (top + 2)],
+                in1=f_sb[:, :, P * lo : P * (top + 1)],
+                op=ALU.subtract,
+            )
+            if hi == R:
+                shifted((dd, R - 1), (f_sb, 0, True), (f_sb, R - 1, False))
+                shifted((dd, R), (f_sb, 1, True), (f_sb, 0, True))
+
+        de = keep.tile([P, 5 * P, T4], BF16)
+        dils = {}
+        codes = {}
+        outs = {}
+
+        def new_window(a):
+            dil = d_pool.tile([P, G, 2 * P, T4], BF16, name="dil", align_bytes=64, bufs=3)
+            dils[a] = dil
+
+        def select_vector(a):
+            lo = a - 1 if a == 1 else a
+            nc.vector.tensor_tensor(
+                out=four_out(de[:, P * lo : P * (a + 2), :]),
+                in0=four(f_sb[:, :, P * (lo + 1) : P * (a + 3)]),
+                in1=four(f_sb[:, :, P * lo : P * (a + 2)]),
+                op=ALU.subtract,
+            )
+            m1 = d_pool.tile([P, 2 * P, T4], BF16, name="m1", bufs=1)
+            m2 = d_pool.tile([P, 2 * P, T4], BF16, name="m2", bufs=1)
+            for s, mm in ((0, m1), (1, m2)):
+                nc.vector.tensor_tensor(
+                    out=mm[:],
+                    in0=de[:, P * (a - 1 + s) : P * (a + 1 + s), :],
+                    in1=selb[:, s : s + 1, :].to_broadcast([P, 2 * P, T4]),
+                    op=ALU.mult,
+                )
+            nc.vector.tensor_tensor(out=dils[a][:, 1, :, :], in0=m1[:], in1=m2[:], op=ALU.add)
+
+        def select_tensor(a, i):
+            bank = ps_t.tile([P, T4, P], F32, name="bank")
+            for t in range(T4):
+                for s in range(2):
+                    nc.tensor.matmul(
+                        bank[:, t, :],
+                        lhsT=diag[:, s, t, :],
+                        rhs=dd[:, t, P * (a + i - 1 + s) : P * (a + i + s)],
+                        start=(s == 0),
+                        stop=(s == 1),
+                    )
+            nc.scalar.copy(out=dils[a][:, 1, P * i : P * (i + 1), :], in_=bank[:].rearrange("p t x -> p x t"))
+
+        def subtract(a):
+            nc.vector.tensor_tensor(
+                out=four_out(dils[a][:, 0, :, :]),
+                in0=four(a_sb[:, :, P * a : P * (a + 2)]),
+                in1=four(a_sb[:, :, P * (a - 1) : P * (a + 1)]),
+                op=ALU.subtract,
+            )
+
+        def quant_d(a):
+            dc = q_pool.tile([P, G, 2 * P], U32, name="dc", align_bytes=64)
+            ds = q_pool.tile([P, G, 2 * P], U8, name="ds", align_bytes=64)
+            nc.vector.quantize_mx(
+                out=dc[:].rearrange("p g x -> p (g x)").bitcast(FP8X4),
+                scales=ds[:].rearrange("p g x -> p (g x)"),
+                in_=dils[a][:].rearrange("p g x t -> p (g x t)"),
+            )
+            codes[a] = (dc, ds)
+
+        def scale_u(a):
+            o = o_pool.tile([P, 2, N], F32, name="o")
+            for i in range(2):
+                nc.scalar.activation(out=o[:, i, :], in_=u_sb[:, a + i - 1, :], func=ACT.Copy, scale=rr[:, a + i : a + i + 1])
+            outs[a] = o
+
+        accs = {}
+
+        def second(a):
+            dc, ds = codes[a]
+            accs[a] = []
+            for i in range(2):
+                acc = ps_o.tile([P, N], F32, name="acc")
+                accs[a].append(acc)
+                for g in range(G):
+                    nc.tensor.matmul_mx(
+                        out=acc[:],
+                        lhsT=dc[:, g, P * i : P * (i + 1)].bitcast(FP8X4),
+                        lhsT_scale=ds[:, g, P * i : P * (i + 1)],
+                        rhs=p_raw[:, g, :].bitcast(FP4X4),
+                        rhs_scale=ps_raw[:, g, :],
+                        start=(g == 0),
+                        stop=(g == G - 1),
+                    )
+
+        def update(a):
+            o = outs[a]
+            for i in range(2):
+                nc.vector.scalar_tensor_tensor(
+                    out=o[:, i, :], in0=accs[a][i][:], scalar=cc[:, a + i : a + i + 1], in1=o[:, i, :], op0=ALU.mult, op1=ALU.add
+                )
+            if a + 1 < R:
+                nc.sync.dma_start(out=out_v[:, a : a + 2, :], in_=o[:])
+            else:
+                nc.sync.dma_start(out=out_v[:, a, :], in_=o[:, 0, :])
+                for lo, hi in ((1, 113), (113, P)):
+                    nc.sync.dma_start(out=out_v[lo:hi, 0, :], in_=o[lo - 1 : hi - 1, 1, :])
+                nc.sync.dma_start(out=out_v[0:1, 0, :], in_=o[P - 1 : P, 1, :])
+
+        ags = {}
+        flux_done = [-1]
+        steps_done = [3]
+
+        def flux_to(a):
+            top = min(a + 1, R - 1)
+            if top > flux_done[0]:
+                flux(flux_done[0] + 1, top)
+                flux_done[0] = top
+
+        def select_front(a):
+            if (a, a + 1) in IL_WINDOWS:
+                select_vector(a)
+            elif a + 1 > steps_done[0]:
+                steps(steps_done[0] + 1, a + 1)
+                steps_done[0] = a + 1
+
+        def turn_all(c):
+            ags[c] = turn(c, widen(c))
+
         w_abs = keep.tile([P, J], F32)
         nc.scalar.activation(out=w_abs[:], in_=w_sb[:], func=ACT.Abs)
         w_cl = keep.tile([P, J], F32)
         nc.vector.tensor_scalar(out=w_cl[:], in0=w_abs[:], scalar1=2.0**-60, scalar2=2.0**60, op0=ALU.max, op1=ALU.min)
-        w_ln = keep.tile([P, J], F32)
-        nc.scalar.activation(out=w_ln[:], in_=w_cl[:], func=ACT.Ln)
-        n_pos = keep.tile([P, J], F32)
-        nc.vector.tensor_scalar(out=n_pos[:], in0=w_sb[:], scalar1=0.0, scalar2=-1.0, op0=ALU.is_gt, op1=ALU.mult)
-        n_neg = keep.tile([P, J], F32)
-        nc.vector.tensor_scalar(out=n_neg[:], in0=w_sb[:], scalar1=0.0, scalar2=-1.0, op0=ALU.is_lt, op1=ALU.mult)
+        nc.scalar.activation(out=w_ln[:, 0:J], in_=w_cl[:], func=ACT.Ln)
+        pen = keep.tile([P, 2 * J], F32)
+        nc.vector.tensor_scalar(out=pen[:, 0:J], in0=w_sb[:], scalar1=0.0, scalar2=-2000.0, op0=ALU.is_le, op1=ALU.mult)
+        nc.vector.tensor_scalar(out=pen[:, J : 2 * J], in0=w_sb[:], scalar1=0.0, scalar2=-2000.0, op0=ALU.is_ge, op1=ALU.mult)
+        for s in range(2):
+            nc.vector.tensor_tensor(
+                out=w_ln[:, J * (s + 1) : J * (s + 2)], in0=w_ln[:, 0:J], in1=pen[:, J * s : J * (s + 1)], op=ALU.add
+            )
 
+        warm_e = keep.tile([P, 1], F32)
+        nc.scalar.activation(out=warm_e[:], in_=warm[:], func=ACT.Exp)
+        turn_all(0)
+        turn_all(1)
+        permute(1)
+        quant_a(0, ags[0])
+        first(0, 1)
+        quant_a(1, ags[1])
+        permute(0)
+        first(1, 1)
+        sel = keep.tile([P, 2, J], F32)
+        nc.vector.tensor_scalar(out=sel[:, 0, :], in0=w_sb[:], scalar1=0.0, scalar2=1.0, op0=ALU.is_gt, op1=ALU.mult)
+        nc.vector.tensor_scalar(out=sel[:, 1, :], in0=w_sb[:], scalar1=0.0, scalar2=-1.0, op0=ALU.is_lt, op1=ALU.mult)
+        selb = keep.tile([P, 2, T4], BF16)
+        nc.vector.tensor_copy(out=selb[:], in_=sel[:, :, T4:J])
+        diag = keep.tile([P, 2, T4, P], BF16)
+
+
+        first(0, 0)
+        for s in range(2):
+            for t in range(T4):
+                nc.gpsimd.tensor_scalar(
+                    out=diag[:, s, t, :], in0=ident[:], scalar1=sel[:, s, T4 + t : T4 + t + 1], scalar2=1.0, op0=ALU.mult, op1=ALU.mult
+                )
+
+
+        turn_all(2)
+        xb3 = widen(3)
+        quant_a(2, ags[2])
+        first(1, 0)
+        new_window(1)
+        select_vector(1)
         one_sg = keep.tile([P, 2 * R], F32)
         nc.vector.tensor_scalar(out=one_sg[:], in0=sg[:], scalar1=1.0, scalar2=None, op0=ALU.add)
         rr = keep.tile([P, 2 * R], F32)
@@ -120,171 +398,40 @@ def tile_entropyclosuremomentkineticupwindstep_d2p_kernel(
         cc = keep.tile([P, 2 * R], F32)
         nc.vector.tensor_scalar(out=cc[:], in0=rr[:], scalar1=-0.5, scalar2=None, op0=ALU.mult)
 
-        m_w = keep.tile([P, J, 2 * P], U8, align_bytes=64)
-        m_s = keep.tile([P, J, P], U8, align_bytes=64)
-        for g in range(G):
-            for t in range(T4):
-                j = T4 * g + t
-                nc.vector.tensor_copy(
-                    out=m_w[:, j, :].rearrange("p (m b) -> p m b", b=2),
-                    in_=m_raw[:, 1024 * g : 1024 * (g + 1)].rearrange("p (m t b) -> p t m b", t=T4, b=2)[:, t, :, :],
-                )
-                nc.gpsimd.tensor_copy(
-                    out=m_s[:, j, :],
-                    in_=ms_raw[:, 512 * g : 512 * (g + 1)].rearrange("p (m t) -> p t m", t=T4)[:, t, :],
-                )
 
-        f_sb = keep.tile([P, J, R, FS], F32)
-        ur = keep.tile([P, R, N], F32)
-
-        def front(c):
-            xb = front_pool.tile([P, RC, N], BF16, name="xb")
-            for r in range(RC):
-                for j in range(4):
-                    src = a_raw[:, RC * c + r, P * j : P * (j + 1)].bitcast(FP8)
-                    dst = xb[:, r, P * j : P * (j + 1)]
-                    if r in WIDEN_SCALAR:
-                        nc.scalar.activation(out=dst, in_=src, func=ACT.Copy, scale=sc[:, j : j + 1])
-                    else:
-                        nc.vector.tensor_scalar(out=dst, in0=src, scalar1=sc[:, j : j + 1], scalar2=None, op0=ALU.mult)
-            ag = front_pool.tile([P, RC * P * T4], BF16, name="ag", align_bytes=64)
-            for h in range(2):
-                bank = ps_t.tile([P, 2, 2, P], F32, name="bank")
-                for rr2 in range(2):
-                    words = xb[:, 2 * h + rr2, :].bitcast(F32)
-                    for v in range(2):
-                        nc.tensor.transpose(bank[:, rr2, v, :], words[:, v : 2 * P : 2], ident[:])
-                nc.scalar.copy(
-                    out=ag[:, 1024 * h : 1024 * (h + 1)].bitcast(F32).rearrange("p (r x v) -> p r x v", r=2, v=2),
-                    in_=bank[:].rearrange("p r v x -> p r x v"),
-                )
-            ac = front_pool.tile([P, RC * P], U32, name="ac", align_bytes=64)
-            asc = front_pool.tile([P, RC * P], U8, name="asc", align_bytes=64)
-            nc.vector.quantize_mx(out=ac[:].bitcast(FP8X4), scales=asc[:], in_=ag[:])
-            return ac, asc
-
-        def first(c, ac, asc):
-            for j in range(J):
-                eta = ps_e.tile([P, RC * P], F32, name="eta")
-                nc.tensor.matmul_mx(
-                    out=eta[:],
-                    lhsT=m_w[:, j, :].bitcast(FP4X4),
-                    lhsT_scale=m_s[:, j, :],
-                    rhs=ac[:].bitcast(FP8X4),
-                    rhs_scale=asc[:],
-                    start=True,
-                    stop=True,
-                )
-                nc.scalar.activation(
-                    out=f_sb[:, j, RC * c : RC * (c + 1), 0:P],
-                    in_=eta[:].rearrange("p (r x) -> p r x", r=RC),
-                    func=ACT.Exp,
-                    bias=w_ln[:, j : j + 1],
-                )
-
-        def diff(a, b, g):
-            nb = b - a + 1
-            d = d_pool.tile([P, T4, 6 * P], BF16, name="d")
-            tts = []
-            for t in range(T4):
-                j = T4 * g + t
-                tt = t_pool.tile([P, 6 * P], F32, name="tt")
-                tts.append(tt)
-                nreg = min(b, R - 2) - a + 1
-                nc.vector.scalar_tensor_tensor(
-                    out=tt[:, 0 : nreg * P].rearrange("p (r x) -> p r x", x=P),
-                    in0=f_sb[:, j, a + 1 : a + nreg + 1, 0:P],
-                    scalar=n_neg[:, j : j + 1],
-                    in1=f_sb[:, j, a : a + nreg, 0:P],
-                    op0=ALU.mult,
-                    op1=ALU.add,
-                )
-                if b == R:
-                    nc.vector.scalar_tensor_tensor(
-                        out=tt[:, nreg * P : (nreg + 1) * P],
-                        in0=f_sb[:, j, 0, 1 : P + 1],
-                        scalar=n_neg[:, j : j + 1],
-                        in1=f_sb[:, j, R - 1, 0:P],
-                        op0=ALU.mult,
-                        op1=ALU.add,
-                    )
-                    nc.vector.scalar_tensor_tensor(
-                        out=tt[:, (nreg + 1) * P : (nreg + 2) * P],
-                        in0=f_sb[:, j, 1, 1 : P + 1],
-                        scalar=n_neg[:, j : j + 1],
-                        in1=f_sb[:, j, 0, 1 : P + 1],
-                        op0=ALU.mult,
-                        op1=ALU.add,
-                    )
-            for t in range(T4):
-                j = T4 * g + t
-                nc.vector.scalar_tensor_tensor(
-                    out=d[:, t, 0 : nb * P].rearrange("p (r x) -> p r x", x=P),
-                    in0=f_sb[:, j, a - 1 : b, 0:P],
-                    scalar=n_pos[:, j : j + 1],
-                    in1=tts[t][:, 0 : nb * P].rearrange("p (r x) -> p r x", x=P),
-                    op0=ALU.mult,
-                    op1=ALU.add,
-                )
-            dil = d_pool.tile([P, 6 * P, T4], BF16, name="dil", align_bytes=64)
-            dc = q_pool.tile([P, 6 * P], U32, name="dc", align_bytes=64)
-            ds = q_pool.tile([P, 6 * P], U8, name="ds", align_bytes=64)
-            for k in range(nb // 2):
-                cols = slice(2 * P * k, 2 * P * (k + 1))
-                dst = dil[:, cols, :].rearrange("p (c i) t -> p c t i", i=4)
-                src = d[:, :, cols].rearrange("p t (c i) -> p c t i", i=4)
-                if (a, g, k) in INTERLEAVE_VECTOR:
-                    nc.vector.tensor_copy(out=dst, in_=src)
-                else:
-                    nc.scalar.copy(out=dst, in_=src)
-                nc.vector.quantize_mx(
-                    out=dc[:, cols].bitcast(FP8X4), scales=ds[:, cols], in_=dil[:, cols, :].rearrange("p x t -> p (x t)")
-                )
-            return dc, ds
-
-        def second(a, b, ops):
-            for k in range((b - a + 1) // 2):
-                o = o_pool.tile([P, 2, N], F32, name="o")
-                for i in range(2):
-                    blk = a + 2 * k + i
-                    cols = slice(P * (2 * k + i), P * (2 * k + i + 1))
-                    acc = ps_o.tile([P, N], F32, name="acc")
-                    for g in range(G):
-                        nc.tensor.matmul_mx(
-                            out=acc[:],
-                            lhsT=ops[g][0][:, cols].bitcast(FP8X4),
-                            lhsT_scale=ops[g][1][:, cols],
-                            rhs=p_raw[:, g, :].bitcast(FP4X4),
-                            rhs_scale=ps_raw[:, g, :],
-                            start=(g == 0),
-                            stop=(g == G - 1),
-                        )
-                    nc.vector.scalar_tensor_tensor(
-                        out=o[:, i, :], in0=acc[:], scalar=cc[:, blk : blk + 1], in1=ur[:, blk - 1, :], op0=ALU.mult, op1=ALU.add
-                    )
-                lo = a + 2 * k
-                if lo + 1 < R:
-                    nc.sync.dma_start(out=out_v[:, lo : lo + 2, :], in_=o[:])
-                else:
-                    nc.sync.dma_start(out=out_v[:, lo, :], in_=o[:, 0, :])
-                    nc.sync.dma_start(out=out_v[1:P, 0, :], in_=o[0 : P - 1, 1, :])
-                    nc.sync.dma_start(out=out_v[0:1, 0, :], in_=o[P - 1 : P, 1, :])
-
-        def scale_u(lo, hi):
-            for i in range(lo, hi):
-                nc.scalar.activation(out=ur[:, i, :], in_=u_sb[:, i, :], func=ACT.Copy, scale=rr[:, i + 1 : i + 2])
-
-        windows = ((1, 2), (3, 6), (7, 10), (11, 16))
-        ac, asc = front(0)
-        first(0, ac, asc)
-        for j in range(J):
-            nc.vector.tensor_copy(out=f_sb[:, j, 0:2, P : P + 1], in_=f_sb[:, j, 0:2, 0:1])
-        for c in range(NCH):
-            if c + 1 < NCH:
-                ac, asc = front(c + 1)
-            a, b = windows[c]
-            scale_u(a - 1, b)
-            ops = [diff(a, b, g) for g in range(G)]
-            if c + 1 < NCH:
-                first(c + 1, ac, asc)
-            second(a, b, ops)
+        ags[3] = turn(3, xb3)
+        xb4 = widen(4)
+        flux_to(1)
+        quant_a(3, ags[3])
+        first(2, 1)
+        scale_u(1)
+        order_w = (1, 3, 5, 7, 9, 11, 15, 13)
+        plan = {0: ((2, 0), (3, 1)), 1: ((3, 0),), 2: ((4, 1),), 3: ((4, 0),)}
+        for k, a in enumerate(order_w):
+            nxt = order_w[k + 1] if k + 1 < len(order_w) else None
+            prev = order_w[k - 1] if k > 0 else None
+            if prev is not None:
+                second(prev)
+            for c, g in plan.get(k, ()):
+                first(c, g)
+            if k == 0:
+                ags[4] = turn(4, xb4)
+                quant_a(4, ags[4])
+            if nxt is not None:
+                new_window(nxt)
+                select_front(nxt)
+            subtract(a)
+            quant_d(a)
+            if nxt is not None and (nxt, nxt + 1) not in IL_WINDOWS:
+                select_tensor(nxt, 0)
+                select_tensor(nxt, 1)
+            if nxt is not None:
+                flux_to(nxt)
+            if prev is not None:
+                update(prev)
+            if k == 0:
+                halo(a_sb, 0, R)
+            if nxt is not None:
+                scale_u(nxt)
+        second(order_w[-1])
+        update(order_w[-1])

@@ -28,6 +28,9 @@ J = G * T4
 WIDEN_SCALAR = ()
 IL_WINDOWS = ((1, 2), (3, 4))
 
+FLUX_TO = {1: 2, 3: 6, 7: 10, 11: 15}
+STEPS_TO = {5: 6, 7: 10, 11: 16}
+
 
 def tile_entropyclosuremomentkineticupwindstep_d2p_kernel(
     tc, alpha_bytes, alpha_scale, m_words, m_scales, w, p_words, p_scales, u, sigma, out
@@ -48,17 +51,17 @@ def tile_entropyclosuremomentkineticupwindstep_d2p_kernel(
         ps_e = ctx.enter_context(tc.psum_pool(name="ps_e", bufs=4))
         ps_o = ctx.enter_context(tc.psum_pool(name="ps_o", bufs=2))
 
+        sc_all = keep.tile([P, 64], F32)
+        nc.scalar.dma_start(out=sc_all[:], in_=alpha_scale.rearrange("i j -> (i j)").partition_broadcast(P))
+        w_sb = keep.tile([P, J], BF16)
+        nc.scalar.dma_start(out=w_sb[:].rearrange("p (g t) -> p g t", t=T4), in_=w.rearrange("(g p t) -> p g t", p=P, t=T4))
         warm = keep.tile([P, 1], F32)
         nc.vector.memset(warm[:], 1.0)
         w_ln = keep.tile([P, 3 * J], F32)
         nc.scalar.activation(out=w_ln[:, 0:1], in_=warm[:], func=ACT.Ln)
 
         a_raw = keep.tile([P, R, N], U8, align_bytes=64)
-        w_sb = keep.tile([P, J], BF16)
-        nc.sync.dma_start(out=w_sb[:].rearrange("p (g t) -> p g t", t=T4), in_=w.rearrange("(g p t) -> p g t", p=P, t=T4))
-        sc_all = keep.tile([P, 64], F32)
-        nc.sync.dma_start(out=sc_all[:], in_=alpha_scale.rearrange("i j -> (i j)").partition_broadcast(P))
-        for lo, hi in CHUNKS[0:1]:
+        for lo, hi in CHUNKS[0:2]:
             nc.sync.dma_start(out=a_raw[:, lo:hi, :], in_=alpha_v[:, lo:hi, :])
         ms_raw = keep.tile([P, Q], U8, align_bytes=64)
         nc.vector.memset(ms_raw[:].bitcast(I32), 0)
@@ -72,7 +75,7 @@ def tile_entropyclosuremomentkineticupwindstep_d2p_kernel(
             )
         ident = keep.tile([P, P], F32)
         make_identity(nc, ident[:])
-        for lo, hi in CHUNKS[1:]:
+        for lo, hi in CHUNKS[2:]:
             nc.sync.dma_start(out=a_raw[:, lo:hi, :], in_=alpha_v[:, lo:hi, :])
         sg = keep.tile([P, 2 * R], BF16)
         nc.sync.dma_start(out=sg[:, 0:R], in_=sigma_v)
@@ -97,10 +100,12 @@ def tile_entropyclosuremomentkineticupwindstep_d2p_kernel(
         m16 = keep.tile([P, R], F32)
         nc.vector.tensor_reduce(out=m16[:], in_=ident[:].rearrange("p (i b) -> p i b", b=8), axis=AX.X, op=ALU.add)
         sc_sel = keep.tile([P, 4, R], F32)
-        for j in range(4):
-            nc.vector.tensor_tensor(
-                out=sc_sel[:, j, :], in0=sc_all[:].rearrange("p (i j) -> p j i", j=4)[:, j, :], in1=m16[:], op=ALU.mult
-            )
+        nc.vector.tensor_tensor(
+            out=sc_sel[:],
+            in0=sc_all[:].rearrange("p (i j) -> p j i", j=4),
+            in1=m16[:].unsqueeze(1).to_broadcast([P, 4, R]),
+            op=ALU.mult,
+        )
         sc = keep.tile([P, 4], F32)
         nc.vector.tensor_reduce(out=sc[:], in_=sc_sel[:], axis=AX.X, op=ALU.add)
 
@@ -156,12 +161,10 @@ def tile_entropyclosuremomentkineticupwindstep_d2p_kernel(
                 out=m_s[:, T4 * g : T4 * (g + 1), :],
                 in_=ms_raw[:, 512 * g : 512 * (g + 1)].rearrange("p (m t) -> p t m", t=T4),
             )
-            for t in range(T4):
-                j = T4 * g + t
-                nc.vector.tensor_copy(
-                    out=m_w[:, j, :].rearrange("p (m b) -> p m b", b=2),
-                    in_=m_raw[:, 1024 * g : 1024 * (g + 1)].rearrange("p (m t b) -> p t m b", t=T4, b=2)[:, t, :, :],
-                )
+            nc.vector.tensor_copy(
+                out=m_w[:, T4 * g : T4 * (g + 1), :].rearrange("p t (m b) -> p t m b", b=2),
+                in_=m_raw[:, 1024 * g : 1024 * (g + 1)].rearrange("p (m t b) -> p t m b", t=T4, b=2),
+            )
 
         def first(c, g):
             lo, hi = CHUNKS[c]
@@ -187,8 +190,8 @@ def tile_entropyclosuremomentkineticupwindstep_d2p_kernel(
                     nc.scalar.activation(out=f_sb[:, t, cols], in_=eta, func=ACT.Exp, bias=w_ln[:, j : j + 1])
 
         def halo(tile_ap, src, dst):
-            nc.vector.tensor_copy(out=tile_ap[:, :, P * dst : P * dst + P - 1], in_=tile_ap[:, :, P * src + 1 : P * (src + 1)])
-            nc.vector.tensor_copy(out=tile_ap[:, :, P * dst + P - 1 : P * (dst + 1)], in_=tile_ap[:, :, P * src : P * src + 1])
+            nc.scalar.copy(out=tile_ap[:, :, P * dst : P * dst + P - 1], in_=tile_ap[:, :, P * src + 1 : P * (src + 1)])
+            nc.scalar.copy(out=tile_ap[:, :, P * dst + P - 1 : P * (dst + 1)], in_=tile_ap[:, :, P * src : P * src + 1])
 
         def shifted(out, in0, in1):
             for dst, src in ((slice(0, P - 1), slice(1, P)), (slice(P - 1, P), slice(0, 1))):
@@ -318,7 +321,10 @@ def tile_entropyclosuremomentkineticupwindstep_d2p_kernel(
                 nc.vector.scalar_tensor_tensor(
                     out=o[:, i, :], in0=accs[a][i][:], scalar=cc[:, a + i : a + i + 1], in1=o[:, i, :], op0=ALU.mult, op1=ALU.add
                 )
-            if a + 1 < R:
+            if a + 1 < R and a == order_w[-1]:
+                for i in range(2):
+                    nc.sync.dma_start(out=out_v[:, a + i, :], in_=o[:, i, :])
+            elif a + 1 < R:
                 nc.sync.dma_start(out=out_v[:, a : a + 2, :], in_=o[:])
             else:
                 nc.sync.dma_start(out=out_v[:, a, :], in_=o[:, 0, :])
@@ -326,12 +332,13 @@ def tile_entropyclosuremomentkineticupwindstep_d2p_kernel(
                     nc.sync.dma_start(out=out_v[lo:hi, 0, :], in_=o[lo - 1 : hi - 1, 1, :])
                 nc.sync.dma_start(out=out_v[0:1, 0, :], in_=o[P - 1 : P, 1, :])
 
+        order_w = (1, 3, 5, 7, 9, 11, 15, 13)
         ags = {}
         flux_done = [-1]
         steps_done = [3]
 
         def flux_to(a):
-            top = min(a + 1, R - 1)
+            top = FLUX_TO.get(a, 0)
             if top > flux_done[0]:
                 flux(flux_done[0] + 1, top)
                 flux_done[0] = top
@@ -339,73 +346,59 @@ def tile_entropyclosuremomentkineticupwindstep_d2p_kernel(
         def select_front(a):
             if (a, a + 1) in IL_WINDOWS:
                 select_vector(a)
-            elif a + 1 > steps_done[0]:
-                steps(steps_done[0] + 1, a + 1)
-                steps_done[0] = a + 1
+            elif STEPS_TO.get(a, 0) > steps_done[0]:
+                steps(steps_done[0] + 1, STEPS_TO[a])
+                steps_done[0] = STEPS_TO[a]
 
-        def turn_all(c):
-            ags[c] = turn(c, widen(c))
+        with tc.manual_schedule(engines={mybir.EngineType.DVE}):
+            w_abs = keep.tile([P, J], F32)
+            w_cl = keep.tile([P, J], F32)
+            pen = keep.tile([P, 2 * J], F32)
+            sel = keep.tile([P, 2, J], F32)
+            selb = keep.tile([P, 2, T4], BF16)
+            diag = keep.tile([P, 2, T4, P], BF16)
+            one_sg = keep.tile([P, 2 * R], F32)
+            rr = keep.tile([P, 2 * R], F32)
+            cc = keep.tile([P, 2 * R], F32)
+            warm_e = keep.tile([P, 1], F32)
 
-        w_abs = keep.tile([P, J], F32)
-        nc.scalar.activation(out=w_abs[:], in_=w_sb[:], func=ACT.Abs)
-        w_cl = keep.tile([P, J], F32)
-        nc.vector.tensor_scalar(out=w_cl[:], in0=w_abs[:], scalar1=2.0**-60, scalar2=2.0**60, op0=ALU.max, op1=ALU.min)
-        nc.scalar.activation(out=w_ln[:, 0:J], in_=w_cl[:], func=ACT.Ln)
-        pen = keep.tile([P, 2 * J], F32)
-        nc.vector.tensor_scalar(out=pen[:, 0:J], in0=w_sb[:], scalar1=0.0, scalar2=-2000.0, op0=ALU.is_le, op1=ALU.mult)
-        nc.vector.tensor_scalar(out=pen[:, J : 2 * J], in0=w_sb[:], scalar1=0.0, scalar2=-2000.0, op0=ALU.is_ge, op1=ALU.mult)
-        for s in range(2):
-            nc.vector.tensor_tensor(
-                out=w_ln[:, J * (s + 1) : J * (s + 2)], in0=w_ln[:, 0:J], in1=pen[:, J * s : J * (s + 1)], op=ALU.add
-            )
-
-        warm_e = keep.tile([P, 1], F32)
-        nc.scalar.activation(out=warm_e[:], in_=warm[:], func=ACT.Exp)
-        turn_all(0)
-        turn_all(1)
-        permute(1)
-        quant_a(0, ags[0])
-        first(0, 1)
-        quant_a(1, ags[1])
-        permute(0)
-        first(1, 1)
-        sel = keep.tile([P, 2, J], F32)
-        nc.vector.tensor_scalar(out=sel[:, 0, :], in0=w_sb[:], scalar1=0.0, scalar2=1.0, op0=ALU.is_gt, op1=ALU.mult)
-        nc.vector.tensor_scalar(out=sel[:, 1, :], in0=w_sb[:], scalar1=0.0, scalar2=-1.0, op0=ALU.is_lt, op1=ALU.mult)
-        selb = keep.tile([P, 2, T4], BF16)
-        nc.vector.tensor_copy(out=selb[:], in_=sel[:, :, T4:J])
-        diag = keep.tile([P, 2, T4, P], BF16)
-
-
-        first(0, 0)
-        for s in range(2):
-            for t in range(T4):
-                nc.gpsimd.tensor_scalar(
-                    out=diag[:, s, t, :], in0=ident[:], scalar1=sel[:, s, T4 + t : T4 + t + 1], scalar2=1.0, op0=ALU.mult, op1=ALU.mult
+            ags[0] = turn(0, widen(0))
+            nc.scalar.activation(out=w_abs[:], in_=w_sb[:], func=ACT.Abs)
+            nc.vector.tensor_scalar(out=w_cl[:], in0=w_abs[:], scalar1=2.0**-60, scalar2=2.0**60, op0=ALU.max, op1=ALU.min)
+            nc.scalar.activation(out=w_ln[:, 0:J], in_=w_cl[:], func=ACT.Ln)
+            nc.scalar.activation(out=warm_e[:], in_=warm[:], func=ACT.Exp)
+            nc.gpsimd.tensor_scalar(out=pen[:, 0:J], in0=w_sb[:], scalar1=0.0, scalar2=-2000.0, op0=ALU.is_le, op1=ALU.mult)
+            nc.gpsimd.tensor_scalar(out=pen[:, J : 2 * J], in0=w_sb[:], scalar1=0.0, scalar2=-2000.0, op0=ALU.is_ge, op1=ALU.mult)
+            nc.gpsimd.tensor_scalar(out=sel[:, 0, :], in0=w_sb[:], scalar1=0.0, scalar2=1.0, op0=ALU.is_gt, op1=ALU.mult)
+            nc.gpsimd.tensor_scalar(out=sel[:, 1, :], in0=w_sb[:], scalar1=0.0, scalar2=-1.0, op0=ALU.is_lt, op1=ALU.mult)
+            nc.gpsimd.tensor_copy(out=selb[:], in_=sel[:, :, T4:J])
+            permute(1)
+            quant_a(0, ags[0])
+            first(0, 1)
+            ags[1] = turn(1, widen(1))
+            for s in range(2):
+                nc.vector.tensor_tensor(
+                    out=w_ln[:, J * (s + 1) : J * (s + 2)], in0=w_ln[:, 0:J], in1=pen[:, J * s : J * (s + 1)], op=ALU.add
                 )
-
-
-        turn_all(2)
-        xb3 = widen(3)
-        quant_a(2, ags[2])
-        first(1, 0)
-        new_window(1)
-        select_vector(1)
-        one_sg = keep.tile([P, 2 * R], F32)
-        nc.vector.tensor_scalar(out=one_sg[:], in0=sg[:], scalar1=1.0, scalar2=None, op0=ALU.add)
-        rr = keep.tile([P, 2 * R], F32)
-        nc.vector.reciprocal(out=rr[:], in_=one_sg[:])
-        cc = keep.tile([P, 2 * R], F32)
-        nc.vector.tensor_scalar(out=cc[:], in0=rr[:], scalar1=-0.5, scalar2=None, op0=ALU.mult)
-
-
-        ags[3] = turn(3, xb3)
-        xb4 = widen(4)
-        flux_to(1)
-        quant_a(3, ags[3])
-        first(2, 1)
-        scale_u(1)
-        order_w = (1, 3, 5, 7, 9, 11, 15, 13)
+            permute(0)
+            quant_a(1, ags[1])
+            first(1, 1)
+            first(0, 0)
+            nc.gpsimd.tensor_scalar(out=one_sg[:], in0=sg[:], scalar1=1.0, scalar2=None, op0=ALU.add)
+            ags[2] = turn(2, widen(2))
+            new_window(1)
+            xb3 = widen(3)
+            select_vector(1)
+            quant_a(2, ags[2])
+            first(1, 0)
+            nc.vector.reciprocal(out=rr[:], in_=one_sg[:])
+            nc.gpsimd.tensor_scalar(out=cc[:], in0=rr[:], scalar1=-0.5, scalar2=None, op0=ALU.mult)
+            ags[3] = turn(3, xb3)
+            xb4 = widen(4)
+            flux_to(1)
+            quant_a(3, ags[3])
+            first(2, 1)
+            scale_u(1)
         plan = {0: ((2, 0), (3, 1)), 1: ((3, 0),), 2: ((4, 1),), 3: ((4, 0),)}
         for k, a in enumerate(order_w):
             nxt = order_w[k + 1] if k + 1 < len(order_w) else None
@@ -417,21 +410,28 @@ def tile_entropyclosuremomentkineticupwindstep_d2p_kernel(
             if k == 0:
                 ags[4] = turn(4, xb4)
                 quant_a(4, ags[4])
+            if k == 0:
+                for s in range(2):
+                    for t in range(T4):
+                        nc.scalar.activation(out=diag[:, s, t, :], in_=ident[:], func=ACT.Copy, scale=sel[:, s, T4 + t : T4 + t + 1])
             if nxt is not None:
                 new_window(nxt)
                 select_front(nxt)
             subtract(a)
-            quant_d(a)
+            if nxt is None:
+                quant_d(a)
+                second(a)
+            if prev is not None:
+                update(prev)
+            if nxt is not None:
+                quant_d(a)
             if nxt is not None and (nxt, nxt + 1) not in IL_WINDOWS:
                 select_tensor(nxt, 0)
                 select_tensor(nxt, 1)
             if nxt is not None:
                 flux_to(nxt)
-            if prev is not None:
-                update(prev)
             if k == 0:
                 halo(a_sb, 0, R)
             if nxt is not None:
                 scale_u(nxt)
-        second(order_w[-1])
         update(order_w[-1])

@@ -20,16 +20,15 @@ ACT = mybir.ActivationFunctionType
 AX = mybir.AxisListType
 
 R = 16
-CHUNKS = ((0, 2), (2, 4), (4, 8), (8, 12), (12, 16))
 G = 2
 T4 = 4
 J = G * T4
-
+CHUNKS = ((0, 4), (4, 8), (8, 12), (12, 16))
+WINDOWS = (1, 3, 5, 7, 9, 11, 15, 13)
+VECTOR_WINDOWS = (1, 3)
+FLUX_TO = {1: 2, 3: 4, 5: 6, 7: 8, 9: 10, 11: 12, 15: 15}
+STEPS_TO = {5: 6, 7: 8, 9: 10, 11: 12, 15: 16}
 WIDEN_SCALAR = ()
-IL_WINDOWS = ((1, 2), (3, 4))
-
-FLUX_TO = {1: 2, 3: 6, 7: 10, 11: 15}
-STEPS_TO = {5: 6, 7: 10, 11: 16}
 
 
 def tile_entropyclosuremomentkineticupwindstep_d2p_kernel(
@@ -44,117 +43,143 @@ def tile_entropyclosuremomentkineticupwindstep_d2p_kernel(
     with ExitStack() as ctx:
         keep = ctx.enter_context(tc.tile_pool(name="keep", bufs=1))
         front_pool = ctx.enter_context(tc.tile_pool(name="front", bufs=2))
-        d_pool = ctx.enter_context(tc.tile_pool(name="dpool", bufs=2))
+        d_pool = ctx.enter_context(tc.tile_pool(name="dpool", bufs=1))
         q_pool = ctx.enter_context(tc.tile_pool(name="qpool", bufs=3))
-        o_pool = ctx.enter_context(tc.tile_pool(name="opool", bufs=4))
+        o_pool = ctx.enter_context(tc.tile_pool(name="opool", bufs=5))
         ps_t = ctx.enter_context(tc.psum_pool(name="ps_t", bufs=2))
         ps_e = ctx.enter_context(tc.psum_pool(name="ps_e", bufs=4))
         ps_o = ctx.enter_context(tc.psum_pool(name="ps_o", bufs=2))
 
         sc_all = keep.tile([P, 64], F32)
-        nc.scalar.dma_start(out=sc_all[:], in_=alpha_scale.rearrange("i j -> (i j)").partition_broadcast(P))
-        w_sb = keep.tile([P, J], BF16)
-        nc.scalar.dma_start(out=w_sb[:].rearrange("p (g t) -> p g t", t=T4), in_=w.rearrange("(g p t) -> p g t", p=P, t=T4))
-        warm = keep.tile([P, 1], F32)
-        nc.vector.memset(warm[:], 1.0)
-        w_ln = keep.tile([P, 3 * J], F32)
-        nc.scalar.activation(out=w_ln[:, 0:1], in_=warm[:], func=ACT.Ln)
-
         a_raw = keep.tile([P, R, N], U8, align_bytes=64)
-        for lo, hi in CHUNKS[0:2]:
-            nc.sync.dma_start(out=a_raw[:, lo:hi, :], in_=alpha_v[:, lo:hi, :])
-        ms_raw = keep.tile([P, Q], U8, align_bytes=64)
-        nc.vector.memset(ms_raw[:].bitcast(I32), 0)
-        ps_raw = keep.tile([P, G, N], U8, align_bytes=64)
-        nc.vector.memset(ps_raw[:].rearrange("p g n -> p (g n)").bitcast(I32), 0)
+        w_sb = keep.tile([P, J], BF16)
         m_raw = keep.tile([P, 2 * Q], U8, align_bytes=64)
+        ms_raw = keep.tile([P, Q], U8, align_bytes=64)
+        ps_raw = keep.tile([P, G, N], U8, align_bytes=64)
+        p_raw = keep.tile([P, G, 2 * N], U8, align_bytes=64)
+        sg = keep.tile([P, R], BF16)
+        sg16 = keep.tile([P, R], BF16)
+        u_sb = keep.tile([P, R, N], BF16)
+        ident = keep.tile([P, P], F32)
+        warm = keep.tile([P, 1], F32)
+        w_ln = keep.tile([P, 3 * J], F32)
+
+        nc.vector.memset(warm[:], 1.0)
+        nc.vector.memset(ms_raw[:].bitcast(I32), 0)
+        nc.vector.memset(ps_raw[:].rearrange("p g n -> p (g n)").bitcast(I32), 0)
+        make_identity(nc, ident[:])
+
+        nc.scalar.dma_start(out=sc_all[:], in_=alpha_scale.rearrange("i j -> (i j)").partition_broadcast(P))
+        nc.scalar.dma_start(out=w_sb[:].rearrange("p (g t) -> p g t", t=T4), in_=w.rearrange("(g p t) -> p g t", p=P, t=T4))
+        nc.sync.dma_start(out=a_raw[:, 0:4, :], in_=alpha_v[:, 0:4, :])
         nc.sync.dma_start(out=m_raw[:].bitcast(I32), in_=m_words[0].bitcast(I32))
         for qd in range(4):
             nc.sync.dma_start(
                 out=ms_raw[32 * qd : 32 * qd + 4, :].bitcast(I32), in_=m_scales[0, 4 * qd : 4 * qd + 4, :].bitcast(I32)
             )
-        ident = keep.tile([P, P], F32)
-        make_identity(nc, ident[:])
-        for lo, hi in CHUNKS[2:]:
+        nc.sync.dma_start(out=sg[:], in_=sigma_v)
+
+        def load_alpha(c):
+            lo, hi = CHUNKS[c]
             nc.sync.dma_start(out=a_raw[:, lo:hi, :], in_=alpha_v[:, lo:hi, :])
-        sg = keep.tile([P, 2 * R], BF16)
-        nc.sync.dma_start(out=sg[:, 0:R], in_=sigma_v)
-        for lo, hi in ((1, 113), (113, P)):
-            nc.sync.dma_start(out=sg[lo - 1 : hi - 1, R : 2 * R], in_=sigma_v[lo:hi, :])
-        nc.sync.dma_start(out=sg[P - 1 : P, R : 2 * R], in_=sigma_v[0:1, :])
-        p_raw = keep.tile([P, G, 2 * N], U8, align_bytes=64)
+
+        load_alpha(1)
+        load_alpha(2)
         for g in range(G):
             nc.sync.dma_start(out=p_raw[:, g, :].bitcast(I32), in_=p_words[g].bitcast(I32))
-        for g in range(G):
-            for qd in range(4):
-                nc.sync.dma_start(
-                    out=ps_raw[32 * qd : 32 * qd + 4, g, :].bitcast(I32), in_=p_scales[g, 4 * qd : 4 * qd + 4, :].bitcast(I32)
-                )
-        u_sb = keep.tile([P, R, N], BF16)
-        for lo, hi in ((1, 5), (5, 9), (9, 13), (13, R)):
+        for qd in range(4):
+            nc.sync.dma_start(
+                out=ps_raw[32 * qd : 32 * qd + 4, :, :].bitcast(I32),
+                in_=p_scales.bitcast(I32)[:, 4 * qd : 4 * qd + 4, :].rearrange("g q n -> q g n"),
+            )
+        nc.sync.dma_start(out=u_sb[:, 0:4, :], in_=u_v[:, 1:5, :])
+        load_alpha(3)
+        for lo, hi in ((5, 9), (9, 13), (13, R)):
             nc.sync.dma_start(out=u_sb[:, lo - 1 : hi - 1, :], in_=u_v[:, lo:hi, :])
         for lo, hi in ((1, 113), (113, P)):
             nc.sync.dma_start(out=u_sb[lo - 1 : hi - 1, R - 1, :], in_=u_v[lo:hi, 0, :])
+            nc.sync.dma_start(out=sg16[lo - 1 : hi - 1, :], in_=sigma_v[lo:hi, :])
         nc.sync.dma_start(out=u_sb[P - 1 : P, R - 1, :], in_=u_v[0:1, 0, :])
+        nc.sync.dma_start(out=sg16[P - 1 : P, :], in_=sigma_v[0:1, :])
 
-        m16 = keep.tile([P, R], F32)
-        nc.vector.tensor_reduce(out=m16[:], in_=ident[:].rearrange("p (i b) -> p i b", b=8), axis=AX.X, op=ALU.add)
-        sc_sel = keep.tile([P, 4, R], F32)
-        nc.vector.tensor_tensor(
-            out=sc_sel[:],
-            in0=sc_all[:].rearrange("p (i j) -> p j i", j=4),
-            in1=m16[:].unsqueeze(1).to_broadcast([P, 4, R]),
-            op=ALU.mult,
-        )
-        sc = keep.tile([P, 4], F32)
-        nc.vector.tensor_reduce(out=sc[:], in_=sc_sel[:], axis=AX.X, op=ALU.add)
+        nc.scalar.activation(out=w_ln[:, 0:1], in_=warm[:], func=ACT.Ln)
 
         a_sb = keep.tile([P, T4, (R + 1) * P], F32)
         b_sb = keep.tile([P, T4, R * P], F32)
         f_sb = keep.tile([P, T4, R * P], F32)
         dd = keep.tile([P, T4, (R + 1) * P], BF16)
-
+        de = keep.tile([P, 5 * P, T4], BF16)
         ac = keep.tile([P, X], U32, align_bytes=64)
         asc = keep.tile([P, X], U8, align_bytes=64)
+        m_w = keep.tile([P, J, 2 * P], U8, align_bytes=64)
+        m_s = keep.tile([P, J, P], U8, align_bytes=64)
+        diag = keep.tile([P, 2, T4, P], BF16)
+        m16 = keep.tile([P, R], F32)
+        sc_sel = keep.tile([P, 4, R], F32)
+        sc = keep.tile([P, 4], F32)
+        w_abs = keep.tile([P, J], F32)
+        w_cl = keep.tile([P, J], F32)
+        pen = keep.tile([P, 2 * J], F32)
+        sel = keep.tile([P, 2, J], F32)
+        selb = keep.tile([P, 2, T4], BF16)
+        one_sg = keep.tile([P, R + 1], F32)
+        rr = keep.tile([P, R + 1], F32)
+        cc = keep.tile([P, R + 1], F32)
+        warm_e = keep.tile([P, 1], F32)
 
-        def widen(c):
+        def scales():
+            nc.vector.tensor_reduce(out=m16[:], in_=ident[:].rearrange("p (i b) -> p i b", b=8), axis=AX.X, op=ALU.add)
+            nc.vector.tensor_tensor(
+                out=sc_sel[:],
+                in0=sc_all[:].rearrange("p (i j) -> p j i", j=4),
+                in1=m16[:].unsqueeze(1).to_broadcast([P, 4, R]),
+                op=ALU.mult,
+            )
+            nc.vector.tensor_reduce(out=sc[:], in_=sc_sel[:], axis=AX.X, op=ALU.add)
+
+        xbs = {}
+        ags = {}
+
+        def widen(c, half=None):
             lo, hi = CHUNKS[c]
-            xb = front_pool.tile([P, 4, N], BF16, name="xb", bufs=4)
-            for r in range(lo, hi):
+            if c not in xbs:
+                xb = front_pool.tile([P, 4, N], BF16, name="xb", bufs=4)
+                xbs[c] = xb
+            rows = range(lo, hi) if half is None else range(lo + 2 * half, lo + 2 * half + 2)
+            for r in rows:
                 for j in range(4):
                     src = a_raw[:, r, P * j : P * (j + 1)].bitcast(FP8)
-                    dst = xb[:, r - lo, P * j : P * (j + 1)]
+                    dst = xbs[c][:, r - lo, P * j : P * (j + 1)]
                     if r in WIDEN_SCALAR:
                         nc.scalar.activation(out=dst, in_=src, func=ACT.Copy, scale=sc[:, j : j + 1])
                     else:
                         nc.vector.tensor_scalar(out=dst, in0=src, scalar1=sc[:, j : j + 1], scalar2=None, op0=ALU.mult)
-            return xb
 
-        def turn(c, xb):
+        def turn(c, half=None):
             lo, hi = CHUNKS[c]
-            ag = front_pool.tile([P, 4 * P * T4], BF16, name="ag", align_bytes=64)
-            for h in range((hi - lo) // 2):
+            if c not in ags:
+                ag = front_pool.tile([P, 4 * P * T4], BF16, name="ag", align_bytes=64)
+                ags[c] = ag
+            halves = range((hi - lo) // 2) if half is None else (half,)
+            for h in halves:
                 bank = ps_t.tile([P, 4, P], F32, name="bank")
                 for i in range(2):
-                    words = xb[:, 2 * h + i, :].bitcast(F32)
+                    words = xbs[c][:, 2 * h + i, :].bitcast(F32)
                     for v in range(2):
                         nc.tensor.transpose(bank[:, 2 * i + v, :], words[:, v : 2 * P : 2], ident[:])
                 nc.scalar.copy(
-                    out=ag[:, 1024 * h : 1024 * (h + 1)].bitcast(F32).rearrange("p (r x v) -> p r x v", r=2, v=2),
+                    out=ags[c][:, 1024 * h : 1024 * (h + 1)].bitcast(F32).rearrange("p (r x v) -> p r x v", r=2, v=2),
                     in_=bank[:].rearrange("p (r v) x -> p r x v", r=2),
                 )
-            return ag
 
-        def quant_a(c, ag):
+        def quant_a(c, half=None):
             lo, hi = CHUNKS[c]
-            nn = (hi - lo) * P
+            b0, b1 = (lo, hi) if half is None else (lo + 2 * half, lo + 2 * half + 2)
             nc.vector.quantize_mx(
-                out=ac[:, P * lo : P * hi].bitcast(FP8X4), scales=asc[:, P * lo : P * hi], in_=ag[:, 0 : T4 * nn]
+                out=ac[:, P * b0 : P * b1].bitcast(FP8X4),
+                scales=asc[:, P * b0 : P * b1],
+                in_=ags[c][:, T4 * P * (b0 - lo) : T4 * P * (b1 - lo)],
             )
-
-
-        m_w = keep.tile([P, J, 2 * P], U8, align_bytes=64)
-        m_s = keep.tile([P, J, P], U8, align_bytes=64)
 
         def permute(g):
             nc.vector.tensor_copy(
@@ -189,10 +214,6 @@ def tile_entropyclosuremomentkineticupwindstep_d2p_kernel(
                 else:
                     nc.scalar.activation(out=f_sb[:, t, cols], in_=eta, func=ACT.Exp, bias=w_ln[:, j : j + 1])
 
-        def halo(tile_ap, src, dst):
-            nc.scalar.copy(out=tile_ap[:, :, P * dst : P * dst + P - 1], in_=tile_ap[:, :, P * src + 1 : P * (src + 1)])
-            nc.scalar.copy(out=tile_ap[:, :, P * dst + P - 1 : P * (dst + 1)], in_=tile_ap[:, :, P * src : P * src + 1])
-
         def shifted(out, in0, in1):
             for dst, src in ((slice(0, P - 1), slice(1, P)), (slice(P - 1, P), slice(0, 1))):
                 pick = []
@@ -200,26 +221,37 @@ def tile_entropyclosuremomentkineticupwindstep_d2p_kernel(
                     ap, blk, moved = operand
                     cols = src if moved else dst
                     pick.append(ap[:, :, P * blk + cols.start : P * blk + cols.stop])
-                nc.vector.tensor_tensor(out=out[0][:, :, P * out[1] + dst.start : P * out[1] + dst.stop], in0=pick[0], in1=pick[1], op=ALU.subtract)
+                nc.vector.tensor_tensor(
+                    out=out[0][:, :, P * out[1] + dst.start : P * out[1] + dst.stop], in0=pick[0], in1=pick[1], op=ALU.subtract
+                )
 
-        def flux(lo, hi):
+        done = {"flux": -1, "steps": 3}
+
+        def halo():
+            nc.scalar.copy(out=a_sb[:, :, P * R : P * R + P - 1], in_=a_sb[:, :, 1:P])
+            nc.scalar.copy(out=a_sb[:, :, P * R + P - 1 : P * (R + 1)], in_=a_sb[:, :, 0:1])
+
+        def flux(hi):
+            lo = done["flux"] + 1
+            if hi < lo:
+                return
+            done["flux"] = hi
             top = min(hi, R - 2)
-            nc.vector.tensor_tensor(
-                out=a_sb[:, :, P * lo : P * (top + 1)],
-                in0=a_sb[:, :, P * lo : P * (top + 1)],
-                in1=b_sb[:, :, P * (lo + 1) : P * (top + 2)],
-                op=ALU.subtract,
-            )
+            if top >= lo:
+                nc.vector.tensor_tensor(
+                    out=a_sb[:, :, P * lo : P * (top + 1)],
+                    in0=a_sb[:, :, P * lo : P * (top + 1)],
+                    in1=b_sb[:, :, P * (lo + 1) : P * (top + 2)],
+                    op=ALU.subtract,
+                )
             if hi == R - 1:
                 shifted((a_sb, R - 1), (a_sb, R - 1, False), (b_sb, 0, True))
 
-        def four(ap):
-            return ap.rearrange("p t (c i) -> p c t i", i=4)
-
-        def four_out(ap):
-            return ap.rearrange("p (c i) t -> p c t i", i=4)
-
-        def steps(lo, hi):
+        def steps(hi):
+            lo = done["steps"] + 1
+            if hi < lo:
+                return
+            done["steps"] = hi
             top = min(hi, R - 2)
             nc.vector.tensor_tensor(
                 out=dd[:, :, P * lo : P * (top + 1)],
@@ -231,16 +263,22 @@ def tile_entropyclosuremomentkineticupwindstep_d2p_kernel(
                 shifted((dd, R - 1), (f_sb, 0, True), (f_sb, R - 1, False))
                 shifted((dd, R), (f_sb, 1, True), (f_sb, 0, True))
 
-        de = keep.tile([P, 5 * P, T4], BF16)
+        def four(ap):
+            return ap.rearrange("p t (c i) -> p c t i", i=4)
+
+        def four_out(ap):
+            return ap.rearrange("p (c i) t -> p c t i", i=4)
+
         dils = {}
         codes = {}
+        accs = {}
         outs = {}
 
         def new_window(a):
             dil = d_pool.tile([P, G, 2 * P, T4], BF16, name="dil", align_bytes=64, bufs=3)
             dils[a] = dil
 
-        def select_vector(a):
+        def vector_steps(a):
             lo = a - 1 if a == 1 else a
             nc.vector.tensor_tensor(
                 out=four_out(de[:, P * lo : P * (a + 2), :]),
@@ -248,29 +286,33 @@ def tile_entropyclosuremomentkineticupwindstep_d2p_kernel(
                 in1=four(f_sb[:, :, P * lo : P * (a + 2)]),
                 op=ALU.subtract,
             )
-            m1 = d_pool.tile([P, 2 * P, T4], BF16, name="m1", bufs=1)
-            m2 = d_pool.tile([P, 2 * P, T4], BF16, name="m2", bufs=1)
-            for s, mm in ((0, m1), (1, m2)):
+
+        def vector_select(a):
+            parts = []
+            for s in range(2):
+                mm = d_pool.tile([P, 2 * P, T4], BF16, name="mm", bufs=2)
+                parts.append(mm)
                 nc.vector.tensor_tensor(
                     out=mm[:],
                     in0=de[:, P * (a - 1 + s) : P * (a + 1 + s), :],
                     in1=selb[:, s : s + 1, :].to_broadcast([P, 2 * P, T4]),
                     op=ALU.mult,
                 )
-            nc.vector.tensor_tensor(out=dils[a][:, 1, :, :], in0=m1[:], in1=m2[:], op=ALU.add)
+            nc.vector.tensor_tensor(out=dils[a][:, 1, :, :], in0=parts[0][:], in1=parts[1][:], op=ALU.add)
 
-        def select_tensor(a, i):
-            bank = ps_t.tile([P, T4, P], F32, name="bank")
-            for t in range(T4):
-                for s in range(2):
-                    nc.tensor.matmul(
-                        bank[:, t, :],
-                        lhsT=diag[:, s, t, :],
-                        rhs=dd[:, t, P * (a + i - 1 + s) : P * (a + i + s)],
-                        start=(s == 0),
-                        stop=(s == 1),
-                    )
-            nc.scalar.copy(out=dils[a][:, 1, P * i : P * (i + 1), :], in_=bank[:].rearrange("p t x -> p x t"))
+        def tensor_select(a):
+            for i in range(2):
+                bank = ps_t.tile([P, T4, P], F32, name="bank")
+                for t in range(T4):
+                    for s in range(2):
+                        nc.tensor.matmul(
+                            bank[:, t, :],
+                            lhsT=diag[:, s, t, :],
+                            rhs=dd[:, t, P * (a + i - 1 + s) : P * (a + i + s)],
+                            start=(s == 0),
+                            stop=(s == 1),
+                        )
+                nc.scalar.copy(out=dils[a][:, 1, P * i : P * (i + 1), :], in_=bank[:].rearrange("p t x -> p x t"))
 
         def subtract(a):
             nc.vector.tensor_tensor(
@@ -296,8 +338,6 @@ def tile_entropyclosuremomentkineticupwindstep_d2p_kernel(
                 nc.scalar.activation(out=o[:, i, :], in_=u_sb[:, a + i - 1, :], func=ACT.Copy, scale=rr[:, a + i : a + i + 1])
             outs[a] = o
 
-        accs = {}
-
         def second(a):
             dc, ds = codes[a]
             accs[a] = []
@@ -321,10 +361,11 @@ def tile_entropyclosuremomentkineticupwindstep_d2p_kernel(
                 nc.vector.scalar_tensor_tensor(
                     out=o[:, i, :], in0=accs[a][i][:], scalar=cc[:, a + i : a + i + 1], in1=o[:, i, :], op0=ALU.mult, op1=ALU.add
                 )
-            if a + 1 < R and a == order_w[-1]:
-                for i in range(2):
+                if a == WINDOWS[-1]:
                     nc.sync.dma_start(out=out_v[:, a + i, :], in_=o[:, i, :])
-            elif a + 1 < R:
+            if a == WINDOWS[-1]:
+                return
+            if a + 1 < R:
                 nc.sync.dma_start(out=out_v[:, a : a + 2, :], in_=o[:])
             else:
                 nc.sync.dma_start(out=out_v[:, a, :], in_=o[:, 0, :])
@@ -332,92 +373,82 @@ def tile_entropyclosuremomentkineticupwindstep_d2p_kernel(
                     nc.sync.dma_start(out=out_v[lo:hi, 0, :], in_=o[lo - 1 : hi - 1, 1, :])
                 nc.sync.dma_start(out=out_v[0:1, 0, :], in_=o[P - 1 : P, 1, :])
 
-        order_w = (1, 3, 5, 7, 9, 11, 15, 13)
-        ags = {}
-        flux_done = [-1]
-        steps_done = [3]
-
-        def flux_to(a):
-            top = FLUX_TO.get(a, 0)
-            if top > flux_done[0]:
-                flux(flux_done[0] + 1, top)
-                flux_done[0] = top
-
-        def select_front(a):
-            if (a, a + 1) in IL_WINDOWS:
-                select_vector(a)
-            elif STEPS_TO.get(a, 0) > steps_done[0]:
-                steps(steps_done[0] + 1, STEPS_TO[a])
-                steps_done[0] = STEPS_TO[a]
-
-        with tc.manual_schedule(engines={mybir.EngineType.DVE}):
-            w_abs = keep.tile([P, J], F32)
-            w_cl = keep.tile([P, J], F32)
-            pen = keep.tile([P, 2 * J], F32)
-            sel = keep.tile([P, 2, J], F32)
-            selb = keep.tile([P, 2, T4], BF16)
-            diag = keep.tile([P, 2, T4, P], BF16)
-            one_sg = keep.tile([P, 2 * R], F32)
-            rr = keep.tile([P, 2 * R], F32)
-            cc = keep.tile([P, 2 * R], F32)
-            warm_e = keep.tile([P, 1], F32)
-
-            ags[0] = turn(0, widen(0))
+        def node_vectors_1():
             nc.scalar.activation(out=w_abs[:], in_=w_sb[:], func=ACT.Abs)
             nc.vector.tensor_scalar(out=w_cl[:], in0=w_abs[:], scalar1=2.0**-60, scalar2=2.0**60, op0=ALU.max, op1=ALU.min)
             nc.scalar.activation(out=w_ln[:, 0:J], in_=w_cl[:], func=ACT.Ln)
             nc.scalar.activation(out=warm_e[:], in_=warm[:], func=ACT.Exp)
-            nc.gpsimd.tensor_scalar(out=pen[:, 0:J], in0=w_sb[:], scalar1=0.0, scalar2=-2000.0, op0=ALU.is_le, op1=ALU.mult)
-            nc.gpsimd.tensor_scalar(out=pen[:, J : 2 * J], in0=w_sb[:], scalar1=0.0, scalar2=-2000.0, op0=ALU.is_ge, op1=ALU.mult)
-            nc.gpsimd.tensor_scalar(out=sel[:, 0, :], in0=w_sb[:], scalar1=0.0, scalar2=1.0, op0=ALU.is_gt, op1=ALU.mult)
-            nc.gpsimd.tensor_scalar(out=sel[:, 1, :], in0=w_sb[:], scalar1=0.0, scalar2=-1.0, op0=ALU.is_lt, op1=ALU.mult)
-            nc.gpsimd.tensor_copy(out=selb[:], in_=sel[:, :, T4:J])
-            permute(1)
-            quant_a(0, ags[0])
-            first(0, 1)
-            ags[1] = turn(1, widen(1))
+
+        def node_vectors_2():
+            nc.vector.tensor_scalar(out=pen[:, 0:J], in0=w_sb[:], scalar1=0.0, scalar2=-2000.0, op0=ALU.is_le, op1=ALU.mult)
+            nc.vector.tensor_scalar(out=pen[:, J : 2 * J], in0=w_sb[:], scalar1=0.0, scalar2=-2000.0, op0=ALU.is_ge, op1=ALU.mult)
+            nc.vector.tensor_scalar(out=sel[:, 0, :], in0=w_sb[:], scalar1=0.0, scalar2=1.0, op0=ALU.is_gt, op1=ALU.mult)
+            nc.vector.tensor_scalar(out=sel[:, 1, :], in0=w_sb[:], scalar1=0.0, scalar2=-1.0, op0=ALU.is_lt, op1=ALU.mult)
             for s in range(2):
                 nc.vector.tensor_tensor(
                     out=w_ln[:, J * (s + 1) : J * (s + 2)], in0=w_ln[:, 0:J], in1=pen[:, J * s : J * (s + 1)], op=ALU.add
                 )
+            nc.vector.tensor_copy(out=selb[:], in_=sel[:, :, T4:J])
+
+        def diagonals():
+            for s in range(2):
+                for t in range(T4):
+                    nc.scalar.activation(out=diag[:, s, t, :], in_=ident[:], func=ACT.Copy, scale=sel[:, s, T4 + t : T4 + t + 1])
+
+        def cell_vectors(cols, src):
+            nc.vector.tensor_scalar(out=one_sg[:, cols], in0=src, scalar1=1.0, scalar2=None, op0=ALU.add)
+            nc.vector.reciprocal(out=rr[:, cols], in_=one_sg[:, cols])
+            nc.vector.tensor_scalar(out=cc[:, cols], in0=rr[:, cols], scalar1=-0.5, scalar2=None, op0=ALU.mult)
+
+        with tc.manual_schedule(engines={mybir.EngineType.DVE}):
+            scales()
+            widen(0, 0)
+            turn(0, 0)
+            widen(0, 1)
+            turn(0, 1)
+            node_vectors_1()
+            permute(1)
+            quant_a(0)
+            first(0, 1)
+            node_vectors_2()
             permute(0)
-            quant_a(1, ags[1])
-            first(1, 1)
             first(0, 0)
-            nc.gpsimd.tensor_scalar(out=one_sg[:], in0=sg[:], scalar1=1.0, scalar2=None, op0=ALU.add)
-            ags[2] = turn(2, widen(2))
+            cell_vectors(slice(0, R), sg[:])
+            widen(1)
+            turn(1)
             new_window(1)
-            xb3 = widen(3)
-            select_vector(1)
-            quant_a(2, ags[2])
-            first(1, 0)
-            nc.vector.reciprocal(out=rr[:], in_=one_sg[:])
-            nc.gpsimd.tensor_scalar(out=cc[:], in0=rr[:], scalar1=-0.5, scalar2=None, op0=ALU.mult)
-            ags[3] = turn(3, xb3)
-            xb4 = widen(4)
-            flux_to(1)
-            quant_a(3, ags[3])
-            first(2, 1)
+            vector_steps(1)
+            quant_a(1)
+            vector_select(1)
             scale_u(1)
-        plan = {0: ((2, 0), (3, 1)), 1: ((3, 0),), 2: ((4, 1),), 3: ((4, 0),)}
-        for k, a in enumerate(order_w):
-            nxt = order_w[k + 1] if k + 1 < len(order_w) else None
-            prev = order_w[k - 1] if k > 0 else None
+            widen(2)
+            turn(2)
+            flux(FLUX_TO[1])
+            quant_a(2)
+            first(1, 1)
+            widen(3)
+        plan = {0: ((1, 0), (2, 1)), 1: ((2, 0),), 2: ((3, 1),), 3: ((3, 0),)}
+        for k, a in enumerate(WINDOWS):
+            prev = WINDOWS[k - 1] if k > 0 else None
+            nxt = WINDOWS[k + 1] if k + 1 < len(WINDOWS) else None
             if prev is not None:
                 second(prev)
             for c, g in plan.get(k, ()):
                 first(c, g)
             if k == 0:
-                ags[4] = turn(4, xb4)
-                quant_a(4, ags[4])
-            if k == 0:
-                for s in range(2):
-                    for t in range(T4):
-                        nc.scalar.activation(out=diag[:, s, t, :], in_=ident[:], func=ACT.Copy, scale=sel[:, s, T4 + t : T4 + t + 1])
+                turn(3)
+                quant_a(3)
             if nxt is not None:
                 new_window(nxt)
-                select_front(nxt)
+                if nxt in VECTOR_WINDOWS:
+                    vector_steps(nxt)
+                else:
+                    steps(STEPS_TO.get(nxt, 0))
+            if k == 0:
+                diagonals()
             subtract(a)
+            if nxt in VECTOR_WINDOWS:
+                vector_select(nxt)
             if nxt is None:
                 quant_d(a)
                 second(a)
@@ -425,13 +456,11 @@ def tile_entropyclosuremomentkineticupwindstep_d2p_kernel(
                 update(prev)
             if nxt is not None:
                 quant_d(a)
-            if nxt is not None and (nxt, nxt + 1) not in IL_WINDOWS:
-                select_tensor(nxt, 0)
-                select_tensor(nxt, 1)
-            if nxt is not None:
-                flux_to(nxt)
-            if k == 0:
-                halo(a_sb, 0, R)
-            if nxt is not None:
+                if nxt not in VECTOR_WINDOWS:
+                    tensor_select(nxt)
+                flux(FLUX_TO.get(nxt, 0))
                 scale_u(nxt)
-        update(order_w[-1])
+            if k == 0:
+                halo()
+                cell_vectors(slice(R, R + 1), sg16[:, 0:1])
+        update(WINDOWS[-1])

@@ -28,7 +28,7 @@ WINDOWS = (1, 3, 5, 7, 9, 11, 15, 13)
 VECTOR_WINDOWS = (1, 3)
 FLUX_TO = {1: 2, 3: 4, 5: 6, 7: 8, 9: 10, 11: 12, 15: 15}
 STEPS_TO = {5: 6, 7: 8, 9: 10, 11: 12, 15: 16}
-WIDEN_SCALAR = ()
+WIDEN_SCALAR = (3,)
 
 
 def tile_entropyclosuremomentkineticupwindstep_d2p_kernel(
@@ -51,7 +51,8 @@ def tile_entropyclosuremomentkineticupwindstep_d2p_kernel(
         ps_o = ctx.enter_context(tc.psum_pool(name="ps_o", bufs=2))
 
         sc_all = keep.tile([P, 64], F32)
-        a_raw = keep.tile([P, R, N], U8, align_bytes=64)
+        a_raw = keep.tile([P, 4, N], U8, align_bytes=64)
+        a_kb = keep.tile([P, 3, 4, 4, P], U8, align_bytes=64)
         w_sb = keep.tile([P, J], BF16)
         m_raw = keep.tile([P, 2 * Q], U8, align_bytes=64)
         ms_raw = keep.tile([P, Q], U8, align_bytes=64)
@@ -71,20 +72,21 @@ def tile_entropyclosuremomentkineticupwindstep_d2p_kernel(
 
         nc.scalar.dma_start(out=sc_all[:], in_=alpha_scale.rearrange("i j -> (i j)").partition_broadcast(P))
         nc.scalar.dma_start(out=w_sb[:].rearrange("p (g t) -> p g t", t=T4), in_=w.rearrange("(g p t) -> p g t", p=P, t=T4))
-        nc.sync.dma_start(out=a_raw[:, 0:4, :], in_=alpha_v[:, 0:4, :])
+        nc.sync.dma_start(out=a_raw[:], in_=alpha_v[:, 0:4, :])
         nc.sync.dma_start(out=m_raw[:].bitcast(I32), in_=m_words[0].bitcast(I32))
         for qd in range(4):
             nc.sync.dma_start(
                 out=ms_raw[32 * qd : 32 * qd + 4, :].bitcast(I32), in_=m_scales[0, 4 * qd : 4 * qd + 4, :].bitcast(I32)
             )
-        nc.sync.dma_start(out=sg[:], in_=sigma_v)
-
         def load_alpha(c):
             lo, hi = CHUNKS[c]
-            nc.sync.dma_start(out=a_raw[:, lo:hi, :], in_=alpha_v[:, lo:hi, :])
+            for j in range(4):
+                nc.sync.dma_start(out=a_kb[:, c - 1, j, :, :], in_=alpha_v[:, lo:hi, P * j : P * (j + 1)])
 
         load_alpha(1)
+        nc.sync.dma_start(out=sg[:], in_=sigma_v)
         load_alpha(2)
+        load_alpha(3)
         for g in range(G):
             nc.sync.dma_start(out=p_raw[:, g, :].bitcast(I32), in_=p_words[g].bitcast(I32))
         for qd in range(4):
@@ -93,7 +95,6 @@ def tile_entropyclosuremomentkineticupwindstep_d2p_kernel(
                 in_=p_scales.bitcast(I32)[:, 4 * qd : 4 * qd + 4, :].rearrange("g q n -> q g n"),
             )
         nc.sync.dma_start(out=u_sb[:, 0:4, :], in_=u_v[:, 1:5, :])
-        load_alpha(3)
         for lo, hi in ((5, 9), (9, 13), (13, R)):
             nc.sync.dma_start(out=u_sb[:, lo - 1 : hi - 1, :], in_=u_v[:, lo:hi, :])
         for lo, hi in ((1, 113), (113, P)):
@@ -145,6 +146,16 @@ def tile_entropyclosuremomentkineticupwindstep_d2p_kernel(
             if c not in xbs:
                 xb = front_pool.tile([P, 4, N], BF16, name="xb", bufs=4)
                 xbs[c] = xb
+            if c > 0:
+                for j in range(4):
+                    nc.vector.tensor_scalar(
+                        out=xbs[c][:, :, P * j : P * (j + 1)],
+                        in0=a_kb[:, c - 1, j, :, :].bitcast(FP8),
+                        scalar1=sc[:, j : j + 1],
+                        scalar2=None,
+                        op0=ALU.mult,
+                    )
+                return
             rows = range(lo, hi) if half is None else range(lo + 2 * half, lo + 2 * half + 2)
             for r in rows:
                 for j in range(4):
@@ -393,7 +404,7 @@ def tile_entropyclosuremomentkineticupwindstep_d2p_kernel(
         def diagonals():
             for s in range(2):
                 for t in range(T4):
-                    nc.scalar.activation(out=diag[:, s, t, :], in_=ident[:], func=ACT.Copy, scale=sel[:, s, T4 + t : T4 + t + 1])
+                    nc.vector.tensor_scalar(out=diag[:, s, t, :], in0=ident[:], scalar1=sel[:, s, T4 + t : T4 + t + 1], scalar2=None, op0=ALU.mult)
 
         def cell_vectors(cols, src):
             nc.vector.tensor_scalar(out=one_sg[:, cols], in0=src, scalar1=1.0, scalar2=None, op0=ALU.add)

from contextlib import ExitStack

import concourse.mybir as mybir
from concourse.masks import make_identity

P = 128
X, N, Q = 2048, 512, 1024
FLOPS = 2 * X * N * Q * 2

F32 = mybir.dt.float32
BF16 = mybir.dt.bfloat16
I32 = mybir.dt.int32
U32 = mybir.dt.uint32
U8 = mybir.dt.uint8
FP8 = mybir.dt.float8_e4m3fn
FP8X4 = mybir.dt.float8_e4m3fn_x4
FP4X4 = mybir.dt.float4_e2m1fn_x4
ALU = mybir.AluOpType
ACT = mybir.ActivationFunctionType
AX = mybir.AxisListType

R = 16
G = 2
T4 = 4
J = G * T4
CHUNKS = ((0, 4), (4, 8), (8, 12), (12, 16))
WINDOWS = (1, 3, 5, 7, 9, 11, 15, 13)
VECTOR_WINDOWS = (1, 3)
FLUX_TO = {1: 2, 3: 4, 5: 6, 7: 8, 9: 10, 11: 12, 15: 15}
STEPS_TO = {5: 6, 7: 8, 9: 10, 11: 12, 15: 16}
WIDEN_SCALAR = (3,)


def tile_entropyclosuremomentkineticupwindstep_d2p_kernel(
    tc, alpha_bytes, alpha_scale, m_words, m_scales, w, p_words, p_scales, u, sigma, out
):
    nc = tc.nc
    alpha_v = alpha_bytes.rearrange("(p r) k -> p r k", r=R)
    u_v = u.rearrange("(p r) n -> p r n", r=R)
    out_v = out.rearrange("(p r) n -> p r n", r=R)
    sigma_v = sigma.rearrange("(p r) -> p r", r=R)

    with ExitStack() as ctx:
        keep = ctx.enter_context(tc.tile_pool(name="keep", bufs=1))
        front_pool = ctx.enter_context(tc.tile_pool(name="front", bufs=2))
        d_pool = ctx.enter_context(tc.tile_pool(name="dpool", bufs=1))
        q_pool = ctx.enter_context(tc.tile_pool(name="qpool", bufs=3))
        o_pool = ctx.enter_context(tc.tile_pool(name="opool", bufs=5))
        ps_t = ctx.enter_context(tc.psum_pool(name="ps_t", bufs=2))
        ps_e = ctx.enter_context(tc.psum_pool(name="ps_e", bufs=4))
        ps_o = ctx.enter_context(tc.psum_pool(name="ps_o", bufs=2))

        sc_all = keep.tile([P, 64], F32)
        a_raw = keep.tile([P, 4, N], U8, align_bytes=64)
        a_kb = keep.tile([P, 3, 4, 4, P], U8, align_bytes=64)
        w_sb = keep.tile([P, J], BF16)
        m_raw = keep.tile([P, 2 * Q], U8, align_bytes=64)
        ms_raw = keep.tile([P, Q], U8, align_bytes=64)
        ps_raw = keep.tile([P, G, N], U8, align_bytes=64)
        p_raw = keep.tile([P, G, 2 * N], U8, align_bytes=64)
        sg = keep.tile([P, R], BF16)
        sg16 = keep.tile([P, R], BF16)
        u_sb = keep.tile([P, R, N], BF16)
        ident = keep.tile([P, P], F32)
        warm = keep.tile([P, 1], F32)
        w_ln = keep.tile([P, 3 * J], F32)

        nc.vector.memset(warm[:], 1.0)
        nc.vector.memset(ms_raw[:].bitcast(I32), 0)
        nc.vector.memset(ps_raw[:].rearrange("p g n -> p (g n)").bitcast(I32), 0)
        make_identity(nc, ident[:])

        nc.scalar.dma_start(out=sc_all[:], in_=alpha_scale.rearrange("i j -> (i j)").partition_broadcast(P))
        nc.scalar.dma_start(out=w_sb[:].rearrange("p (g t) -> p g t", t=T4), in_=w.rearrange("(g p t) -> p g t", p=P, t=T4))
        nc.sync.dma_start(out=a_raw[:], in_=alpha_v[:, 0:4, :])
        nc.sync.dma_start(out=m_raw[:].bitcast(I32), in_=m_words[0].bitcast(I32))
        for qd in range(4):
            nc.sync.dma_start(
                out=ms_raw[32 * qd : 32 * qd + 4, :].bitcast(I32), in_=m_scales[0, 4 * qd : 4 * qd + 4, :].bitcast(I32)
            )
        def load_alpha(c):
            lo, hi = CHUNKS[c]
            for j in range(4):
                nc.sync.dma_start(out=a_kb[:, c - 1, j, :, :], in_=alpha_v[:, lo:hi, P * j : P * (j + 1)])

        load_alpha(1)
        nc.sync.dma_start(out=sg[:], in_=sigma_v)
        load_alpha(2)
        load_alpha(3)
        for g in range(G):
            nc.sync.dma_start(out=p_raw[:, g, :].bitcast(I32), in_=p_words[g].bitcast(I32))
        for qd in range(4):
            nc.sync.dma_start(
                out=ps_raw[32 * qd : 32 * qd + 4, :, :].bitcast(I32),
                in_=p_scales.bitcast(I32)[:, 4 * qd : 4 * qd + 4, :].rearrange("g q n -> q g n"),
            )
        nc.sync.dma_start(out=u_sb[:, 0:4, :], in_=u_v[:, 1:5, :])
        for lo, hi in ((5, 9), (9, 13), (13, R)):
            nc.sync.dma_start(out=u_sb[:, lo - 1 : hi - 1, :], in_=u_v[:, lo:hi, :])
        for lo, hi in ((1, 113), (113, P)):
            nc.sync.dma_start(out=u_sb[lo - 1 : hi - 1, R - 1, :], in_=u_v[lo:hi, 0, :])
            nc.sync.dma_start(out=sg16[lo - 1 : hi - 1, :], in_=sigma_v[lo:hi, :])
        nc.sync.dma_start(out=u_sb[P - 1 : P, R - 1, :], in_=u_v[0:1, 0, :])
        nc.sync.dma_start(out=sg16[P - 1 : P, :], in_=sigma_v[0:1, :])

        nc.scalar.activation(out=w_ln[:, 0:1], in_=warm[:], func=ACT.Ln)

        a_sb = keep.tile([P, T4, (R + 1) * P], F32)
        b_sb = keep.tile([P, T4, R * P], F32)
        f_sb = keep.tile([P, T4, R * P], F32)
        dd = keep.tile([P, T4, (R + 1) * P], BF16)
        de = keep.tile([P, 5 * P, T4], BF16)
        ac = keep.tile([P, X], U32, align_bytes=64)
        asc = keep.tile([P, X], U8, align_bytes=64)
        m_w = keep.tile([P, J, 2 * P], U8, align_bytes=64)
        m_s = keep.tile([P, J, P], U8, align_bytes=64)
        diag = keep.tile([P, 2, T4, P], BF16)
        m16 = keep.tile([P, R], F32)
        sc_sel = keep.tile([P, 4, R], F32)
        sc = keep.tile([P, 4], F32)
        w_abs = keep.tile([P, J], F32)
        w_cl = keep.tile([P, J], F32)
        pen = keep.tile([P, 2 * J], F32)
        sel = keep.tile([P, 2, J], F32)
        selb = keep.tile([P, 2, T4], BF16)
        one_sg = keep.tile([P, R + 1], F32)
        rr = keep.tile([P, R + 1], F32)
        cc = keep.tile([P, R + 1], F32)
        warm_e = keep.tile([P, 1], F32)

        def scales():
            nc.vector.tensor_reduce(out=m16[:], in_=ident[:].rearrange("p (i b) -> p i b", b=8), axis=AX.X, op=ALU.add)
            nc.vector.tensor_tensor(
                out=sc_sel[:],
                in0=sc_all[:].rearrange("p (i j) -> p j i", j=4),
                in1=m16[:].unsqueeze(1).to_broadcast([P, 4, R]),
                op=ALU.mult,
            )
            nc.vector.tensor_reduce(out=sc[:], in_=sc_sel[:], axis=AX.X, op=ALU.add)

        xbs = {}
        ags = {}

        def widen(c, half=None):
            lo, hi = CHUNKS[c]
            if c not in xbs:
                xb = front_pool.tile([P, 4, N], BF16, name="xb", bufs=4)
                xbs[c] = xb
            if c > 0:
                for j in range(4):
                    nc.vector.tensor_scalar(
                        out=xbs[c][:, :, P * j : P * (j + 1)],
                        in0=a_kb[:, c - 1, j, :, :].bitcast(FP8),
                        scalar1=sc[:, j : j + 1],
                        scalar2=None,
                        op0=ALU.mult,
                    )
                return
            rows = range(lo, hi) if half is None else range(lo + 2 * half, lo + 2 * half + 2)
            for r in rows:
                for j in range(4):
                    src = a_raw[:, r, P * j : P * (j + 1)].bitcast(FP8)
                    dst = xbs[c][:, r - lo, P * j : P * (j + 1)]
                    if r in WIDEN_SCALAR:
                        nc.scalar.activation(out=dst, in_=src, func=ACT.Copy, scale=sc[:, j : j + 1])
                    else:
                        nc.vector.tensor_scalar(out=dst, in0=src, scalar1=sc[:, j : j + 1], scalar2=None, op0=ALU.mult)

        def turn(c, half=None):
            lo, hi = CHUNKS[c]
            if c not in ags:
                ag = front_pool.tile([P, 4 * P * T4], BF16, name="ag", align_bytes=64)
                ags[c] = ag
            halves = range((hi - lo) // 2) if half is None else (half,)
            for h in halves:
                bank = ps_t.tile([P, 4, P], F32, name="bank")
                for i in range(2):
                    words = xbs[c][:, 2 * h + i, :].bitcast(F32)
                    for v in range(2):
                        nc.tensor.transpose(bank[:, 2 * i + v, :], words[:, v : 2 * P : 2], ident[:])
                nc.scalar.copy(
                    out=ags[c][:, 1024 * h : 1024 * (h + 1)].bitcast(F32).rearrange("p (r x v) -> p r x v", r=2, v=2),
                    in_=bank[:].rearrange("p (r v) x -> p r x v", r=2),
                )

        def quant_a(c, half=None):
            lo, hi = CHUNKS[c]
            b0, b1 = (lo, hi) if half is None else (lo + 2 * half, lo + 2 * half + 2)
            nc.vector.quantize_mx(
                out=ac[:, P * b0 : P * b1].bitcast(FP8X4),
                scales=asc[:, P * b0 : P * b1],
                in_=ags[c][:, T4 * P * (b0 - lo) : T4 * P * (b1 - lo)],
            )

        def permute(g):
            nc.vector.tensor_copy(
                out=m_s[:, T4 * g : T4 * (g + 1), :],
                in_=ms_raw[:, 512 * g : 512 * (g + 1)].rearrange("p (m t) -> p t m", t=T4),
            )
            nc.vector.tensor_copy(
                out=m_w[:, T4 * g : T4 * (g + 1), :].rearrange("p t (m b) -> p t m b", b=2),
                in_=m_raw[:, 1024 * g : 1024 * (g + 1)].rearrange("p (m t b) -> p t m b", t=T4, b=2),
            )

        def first(c, g):
            lo, hi = CHUNKS[c]
            nn = (hi - lo) * P
            cols = slice(P * lo, P * hi)
            for t in range(T4):
                j = T4 * g + t
                bank_e = ps_e.tile([P, 4 * P], F32, name="bank_e")
                eta = bank_e[:, 0:nn]
                nc.tensor.matmul_mx(
                    out=eta,
                    lhsT=m_w[:, j, :].bitcast(FP4X4),
                    lhsT_scale=m_s[:, j, :],
                    rhs=ac[:, cols].bitcast(FP8X4),
                    rhs_scale=asc[:, cols],
                    start=True,
                    stop=True,
                )
                if g == 0:
                    nc.scalar.activation(out=a_sb[:, t, cols], in_=eta, func=ACT.Exp, bias=w_ln[:, J + t : J + t + 1])
                    nc.scalar.activation(out=b_sb[:, t, cols], in_=eta, func=ACT.Exp, bias=w_ln[:, 2 * J + t : 2 * J + t + 1])
                else:
                    nc.scalar.activation(out=f_sb[:, t, cols], in_=eta, func=ACT.Exp, bias=w_ln[:, j : j + 1])

        def shifted(out, in0, in1):
            for dst, src in ((slice(0, P - 1), slice(1, P)), (slice(P - 1, P), slice(0, 1))):
                pick = []
                for operand in (in0, in1):
                    ap, blk, moved = operand
                    cols = src if moved else dst
                    pick.append(ap[:, :, P * blk + cols.start : P * blk + cols.stop])
                nc.vector.tensor_tensor(
                    out=out[0][:, :, P * out[1] + dst.start : P * out[1] + dst.stop], in0=pick[0], in1=pick[1], op=ALU.subtract
                )

        done = {"flux": -1, "steps": 3}

        def halo():
            nc.scalar.copy(out=a_sb[:, :, P * R : P * R + P - 1], in_=a_sb[:, :, 1:P])
            nc.scalar.copy(out=a_sb[:, :, P * R + P - 1 : P * (R + 1)], in_=a_sb[:, :, 0:1])

        def flux(hi):
            lo = done["flux"] + 1
            if hi < lo:
                return
            done["flux"] = hi
            top = min(hi, R - 2)
            if top >= lo:
                nc.vector.tensor_tensor(
                    out=a_sb[:, :, P * lo : P * (top + 1)],
                    in0=a_sb[:, :, P * lo : P * (top + 1)],
                    in1=b_sb[:, :, P * (lo + 1) : P * (top + 2)],
                    op=ALU.subtract,
                )
            if hi == R - 1:
                shifted((a_sb, R - 1), (a_sb, R - 1, False), (b_sb, 0, True))

        def steps(hi):
            lo = done["steps"] + 1
            if hi < lo:
                return
            done["steps"] = hi
            top = min(hi, R - 2)
            nc.vector.tensor_tensor(
                out=dd[:, :, P * lo : P * (top + 1)],
                in0=f_sb[:, :, P * (lo + 1) : P * (top + 2)],
                in1=f_sb[:, :, P * lo : P * (top + 1)],
                op=ALU.subtract,
            )
            if hi == R:
                shifted((dd, R - 1), (f_sb, 0, True), (f_sb, R - 1, False))
                shifted((dd, R), (f_sb, 1, True), (f_sb, 0, True))

        def four(ap):
            return ap.rearrange("p t (c i) -> p c t i", i=4)

        def four_out(ap):
            return ap.rearrange("p (c i) t -> p c t i", i=4)

        dils = {}
        codes = {}
        accs = {}
        outs = {}

        def new_window(a):
            dil = d_pool.tile([P, G, 2 * P, T4], BF16, name="dil", align_bytes=64, bufs=3)
            dils[a] = dil

        def vector_steps(a):
            lo = a - 1 if a == 1 else a
            nc.vector.tensor_tensor(
                out=four_out(de[:, P * lo : P * (a + 2), :]),
                in0=four(f_sb[:, :, P * (lo + 1) : P * (a + 3)]),
                in1=four(f_sb[:, :, P * lo : P * (a + 2)]),
                op=ALU.subtract,
            )

        def vector_select(a):
            parts = []
            for s in range(2):
                mm = d_pool.tile([P, 2 * P, T4], BF16, name="mm", bufs=2)
                parts.append(mm)
                nc.vector.tensor_tensor(
                    out=mm[:],
                    in0=de[:, P * (a - 1 + s) : P * (a + 1 + s), :],
                    in1=selb[:, s : s + 1, :].to_broadcast([P, 2 * P, T4]),
                    op=ALU.mult,
                )
            nc.vector.tensor_tensor(out=dils[a][:, 1, :, :], in0=parts[0][:], in1=parts[1][:], op=ALU.add)

        def tensor_select(a):
            for i in range(2):
                bank = ps_t.tile([P, T4, P], F32, name="bank")
                for t in range(T4):
                    for s in range(2):
                        nc.tensor.matmul(
                            bank[:, t, :],
                            lhsT=diag[:, s, t, :],
                            rhs=dd[:, t, P * (a + i - 1 + s) : P * (a + i + s)],
                            start=(s == 0),
                            stop=(s == 1),
                        )
                nc.scalar.copy(out=dils[a][:, 1, P * i : P * (i + 1), :], in_=bank[:].rearrange("p t x -> p x t"))

        def subtract(a):
            nc.vector.tensor_tensor(
                out=four_out(dils[a][:, 0, :, :]),
                in0=four(a_sb[:, :, P * a : P * (a + 2)]),
                in1=four(a_sb[:, :, P * (a - 1) : P * (a + 1)]),
                op=ALU.subtract,
            )

        def quant_d(a):
            dc = q_pool.tile([P, G, 2 * P], U32, name="dc", align_bytes=64)
            ds = q_pool.tile([P, G, 2 * P], U8, name="ds", align_bytes=64)
            nc.vector.quantize_mx(
                out=dc[:].rearrange("p g x -> p (g x)").bitcast(FP8X4),
                scales=ds[:].rearrange("p g x -> p (g x)"),
                in_=dils[a][:].rearrange("p g x t -> p (g x t)"),
            )
            codes[a] = (dc, ds)

        def scale_u(a):
            o = o_pool.tile([P, 2, N], F32, name="o")
            for i in range(2):
                nc.scalar.activation(out=o[:, i, :], in_=u_sb[:, a + i - 1, :], func=ACT.Copy, scale=rr[:, a + i : a + i + 1])
            outs[a] = o

        def second(a):
            dc, ds = codes[a]
            accs[a] = []
            for i in range(2):
                acc = ps_o.tile([P, N], F32, name="acc")
                accs[a].append(acc)
                for g in range(G):
                    nc.tensor.matmul_mx(
                        out=acc[:],
                        lhsT=dc[:, g, P * i : P * (i + 1)].bitcast(FP8X4),
                        lhsT_scale=ds[:, g, P * i : P * (i + 1)],
                        rhs=p_raw[:, g, :].bitcast(FP4X4),
                        rhs_scale=ps_raw[:, g, :],
                        start=(g == 0),
                        stop=(g == G - 1),
                    )

        def update(a):
            o = outs[a]
            for i in range(2):
                nc.vector.scalar_tensor_tensor(
                    out=o[:, i, :], in0=accs[a][i][:], scalar=cc[:, a + i : a + i + 1], in1=o[:, i, :], op0=ALU.mult, op1=ALU.add
                )
                if a == WINDOWS[-1]:
                    nc.sync.dma_start(out=out_v[:, a + i, :], in_=o[:, i, :])
            if a == WINDOWS[-1]:
                return
            if a + 1 < R:
                nc.sync.dma_start(out=out_v[:, a : a + 2, :], in_=o[:])
            else:
                nc.sync.dma_start(out=out_v[:, a, :], in_=o[:, 0, :])
                for lo, hi in ((1, 113), (113, P)):
                    nc.sync.dma_start(out=out_v[lo:hi, 0, :], in_=o[lo - 1 : hi - 1, 1, :])
                nc.sync.dma_start(out=out_v[0:1, 0, :], in_=o[P - 1 : P, 1, :])

        def node_vectors_1():
            nc.scalar.activation(out=w_abs[:], in_=w_sb[:], func=ACT.Abs)
            nc.vector.tensor_scalar(out=w_cl[:], in0=w_abs[:], scalar1=2.0**-60, scalar2=2.0**60, op0=ALU.max, op1=ALU.min)
            nc.scalar.activation(out=w_ln[:, 0:J], in_=w_cl[:], func=ACT.Ln)
            nc.scalar.activation(out=warm_e[:], in_=warm[:], func=ACT.Exp)

        def node_vectors_2():
            nc.vector.tensor_scalar(out=pen[:, 0:J], in0=w_sb[:], scalar1=0.0, scalar2=-2000.0, op0=ALU.is_le, op1=ALU.mult)
            nc.vector.tensor_scalar(out=pen[:, J : 2 * J], in0=w_sb[:], scalar1=0.0, scalar2=-2000.0, op0=ALU.is_ge, op1=ALU.mult)
            nc.vector.tensor_scalar(out=sel[:, 0, :], in0=w_sb[:], scalar1=0.0, scalar2=1.0, op0=ALU.is_gt, op1=ALU.mult)
            nc.vector.tensor_scalar(out=sel[:, 1, :], in0=w_sb[:], scalar1=0.0, scalar2=-1.0, op0=ALU.is_lt, op1=ALU.mult)
            for s in range(2):
                nc.vector.tensor_tensor(
                    out=w_ln[:, J * (s + 1) : J * (s + 2)], in0=w_ln[:, 0:J], in1=pen[:, J * s : J * (s + 1)], op=ALU.add
                )
            nc.vector.tensor_copy(out=selb[:], in_=sel[:, :, T4:J])

        def diagonals():
            for s in range(2):
                for t in range(T4):
                    nc.vector.tensor_scalar(out=diag[:, s, t, :], in0=ident[:], scalar1=sel[:, s, T4 + t : T4 + t + 1], scalar2=None, op0=ALU.mult)

        def cell_vectors(cols, src):
            nc.vector.tensor_scalar(out=one_sg[:, cols], in0=src, scalar1=1.0, scalar2=None, op0=ALU.add)
            nc.vector.reciprocal(out=rr[:, cols], in_=one_sg[:, cols])
            nc.vector.tensor_scalar(out=cc[:, cols], in0=rr[:, cols], scalar1=-0.5, scalar2=None, op0=ALU.mult)

        with tc.manual_schedule(engines={mybir.EngineType.DVE}):
            scales()
            widen(0, 0)
            turn(0, 0)
            widen(0, 1)
            turn(0, 1)
            node_vectors_1()
            permute(1)
            quant_a(0)
            first(0, 1)
            node_vectors_2()
            permute(0)
            first(0, 0)
            cell_vectors(slice(0, R), sg[:])
            widen(1)
            turn(1)
            new_window(1)
            vector_steps(1)
            quant_a(1)
            vector_select(1)
            scale_u(1)
            widen(2)
            turn(2)
            flux(FLUX_TO[1])
            quant_a(2)
            first(1, 1)
            widen(3)
        plan = {0: ((1, 0), (2, 1)), 1: ((2, 0),), 2: ((3, 1),), 3: ((3, 0),)}
        for k, a in enumerate(WINDOWS):
            prev = WINDOWS[k - 1] if k > 0 else None
            nxt = WINDOWS[k + 1] if k + 1 < len(WINDOWS) else None
            if prev is not None:
                second(prev)
            for c, g in plan.get(k, ()):
                first(c, g)
            if k == 0:
                turn(3)
                quant_a(3)
            if nxt is not None:
                new_window(nxt)
                if nxt in VECTOR_WINDOWS:
                    vector_steps(nxt)
                else:
                    steps(STEPS_TO.get(nxt, 0))
            if k == 0:
                diagonals()
            subtract(a)
            if nxt in VECTOR_WINDOWS:
                vector_select(nxt)
            if nxt is None:
                quant_d(a)
                second(a)
            if prev is not None:
                update(prev)
            if nxt is not None:
                quant_d(a)
                if nxt not in VECTOR_WINDOWS:
                    tensor_select(nxt)
                flux(FLUX_TO.get(nxt, 0))
                scale_u(nxt)
            if k == 0:
                halo()
                cell_vectors(slice(R, R + 1), sg16[:, 0:1])
        update(WINDOWS[-1])
